import numpy as np
import ml_dtypes


def mxq(x, axis, fmt="e4m3"):
    dtype, down = {"e4m3": (ml_dtypes.float8_e4m3fn, 7), "e5m2": (ml_dtypes.float8_e5m2, 14)}[fmt]
    v = np.moveaxis(np.asarray(x, np.float32).astype(ml_dtypes.bfloat16).astype(np.float64), axis, -1)
    blocks = v.reshape(v.shape[:-1] + (-1, 32))
    amax = np.abs(blocks).max(-1, keepdims=True)
    byte = np.maximum(np.where(amax > 0, np.frexp(amax)[1] - 1 + 127, 0) - down, 1)
    scale = np.exp2(byte - 127.0)
    codes = (blocks / scale).astype(np.float32).astype(dtype).astype(np.float64)
    return np.moveaxis((codes * scale).reshape(v.shape), -1, axis)


WIDE = False


def mx_kscale(k):
    if not WIDE:
        return np.ones(k)
    levels = np.array([10, -10, 5, -5, 0])
    if k % 512:
        return np.exp2(np.random.permutation(np.resize(levels, k // 32))).repeat(32)
    a = np.empty((k // 512, 16))
    for p in range(k // 512):
        a[p, :8] = np.random.permutation(np.resize(levels, 8))
        for g in range(8):
            far = levels[np.abs(levels - a[p, g]) >= 10]
            a[p, g + 8] = far[np.random.randint(len(far))]
    return np.exp2(a.ravel()).repeat(32)


def f64(x):
    return np.asarray(x).astype(np.float64)


def striped(idx):
    return np.tile(idx.reshape(-1, 16).T, (8, 1)).astype(np.uint16)


def unstriped(offs):
    return offs[:16].T.reshape(-1).astype(np.int64)


E2M1 = np.array([0.0, 0.5, 1.0, 1.5, 2.0, 3.0, 4.0, 6.0, -0.0, -0.5, -1.0, -1.5, -2.0, -3.0, -4.0, -6.0])


def pack_weight(w, fmt):
    k, n = w.shape
    w = f64(np.asarray(w, np.float32).astype(ml_dtypes.bfloat16)).reshape(k // 32, 32, n)
    amax = np.abs(w).max(1)
    if fmt == "e4m3":
        byte = np.frexp(amax)[1] - 1 + 127 - 7
    else:
        mant, ex = np.frexp(amax / 6.0)
        byte = np.where(mant > 0.5, ex, ex - 1) + 127
    byte = np.clip(np.where(amax > 0, byte, 1), 1, 254)
    scaled = (w * np.exp2(127.0 - byte)[:, None, :]).reshape(k, n).astype(np.float32)
    by_word = np.ascontiguousarray(scaled.reshape(k // 512, 128, 4, n).transpose(0, 1, 3, 2))
    if fmt == "e4m3":
        words = by_word.astype(ml_dtypes.float8_e4m3fn).view(np.uint8)
    else:
        c = by_word.astype(ml_dtypes.float4_e2m1fn).view(np.uint8) & 0xF
        words = (c[..., 0::2] | (c[..., 1::2] << 4)).reshape(k // 512, 128, 2 * n)
    return np.ascontiguousarray(words), np.ascontiguousarray(byte.astype(np.uint8).reshape(k // 512, 16, n))


def unpack_weight(words, scales, fmt):
    g, _, n = scales.shape
    words = np.ascontiguousarray(words).reshape(g, 128, n, -1)
    if fmt == "e4m3":
        vals = words.view(ml_dtypes.float8_e4m3fn).astype(np.float64)
    else:
        nib = np.empty((g, 128, n, 4), np.uint8)
        nib[..., 0::2] = words & 0xF
        nib[..., 1::2] = words >> 4
        vals = E2M1[nib]
    vals = vals * np.repeat(np.exp2(scales.astype(np.float64) - 127.0), 8, axis=1)[..., None]
    return vals.transpose(0, 1, 3, 2).reshape(g * 512, n)


def relu(v):
    return np.maximum(v, 0.0)


K, T, E, C, H, N = 2048, 640, 6, 128, 512, 384
R = 2


def by_expert(wq, xq):
    return np.concatenate([wq[e].T @ xq[:, e * C:(e + 1) * C] for e in range(E)], axis=1)


def setup_inputs():
    n = np.random.standard_normal
    s = mx_kscale(K)[:, None]
    u = mx_kscale(H)
    slot_token = np.concatenate([r * (T // R) + np.random.permutation(T // R)[:C // R] for e in range(E) for r in range(R)])
    w1 = [pack_weight(m, "e2m1") for m in n((E, K, H)) / np.sqrt(K) / s[None] * u[None, None, :]]
    w2 = [pack_weight(m, "e2m1") for m in n((E, H, N)) / np.sqrt(H) / u[None, :, None]]
    return {
        "xT": (n((K, T)) * s).astype(np.float32),
        "w1_words": np.stack([m[0] for m in w1]),
        "w1_scales": np.stack([m[1] for m in w1]),
        "w2_words": np.stack([m[0] for m in w2]),
        "w2_scales": np.stack([m[1] for m in w2]),
        "offs": striped(slot_token),
    }


def reference(xT, w1_words, w1_scales, w2_words, w2_scales, offs):
    idx = unstriped(offs)
    w1 = np.stack([unpack_weight(w1_words[e], w1_scales[e], "e2m1") for e in range(E)])
    w2 = np.stack([unpack_weight(w2_words[e], w2_scales[e], "e2m1") for e in range(E)])
    xq = mxq(f64(xT)[:, idx], 0, "e4m3")
    h = relu(by_expert(w1, xq))
    y = by_expert(w2, mxq(h, 0, "e4m3"))
    return y.reshape(N, E, R, C // R).transpose(0, 2, 1, 3).reshape(N, E * C)

@@ -1,0 +1,196 @@
+from contextlib import ExitStack
+
+import concourse.mybir as mybir
+from concourse.masks import make_identity
+
+K, T, E, C, H, N = 2048, 640, 6, 128, 512, 384
+RANKS = 2
+P = 128
+PASSES = K // 512
+SLOTS = E * C
+U = C // RANKS
+FLOPS = 2 * SLOTS * (K * H + H * N)
+
+F32 = mybir.dt.float32
+BF16 = mybir.dt.bfloat16
+I32 = mybir.dt.int32
+U32 = mybir.dt.uint32
+U16 = mybir.dt.uint16
+U8 = mybir.dt.uint8
+FP8X4 = mybir.dt.float8_e4m3fn_x4
+FP4X4 = mybir.dt.float4_e2m1fn_x4
+RELU = mybir.ActivationFunctionType.Relu
+
+
+def tile_moe_eps_mlp_relu_kernel(tc, xT, w1_words, w1_scales, w2_words, w2_scales, offs, out):
+    nc = tc.nc
+    with ExitStack() as ctx:
+        keep = ctx.enter_context(tc.tile_pool(name="keep", bufs=1))
+        psum = ctx.enter_context(tc.psum_pool(name="psum", bufs=1))
+
+        offsets = keep.tile([P, SLOTS // 16], U16, name="offsets")
+        x_raw = [keep.tile([P, 4, T], F32, name=f"x_raw{s}") for s in range(PASSES)]
+        x_bf = [keep.tile([P, T, 4], BF16, name=f"x_bf{s}", align_bytes=64) for s in range(PASSES)]
+        t_codes = [keep.tile([P, T], U32, name=f"t_codes{s}", align_bytes=64) for s in range(PASSES)]
+        t_scales = [keep.tile([P, T], U8, name=f"t_scales{s}", align_bytes=64) for s in range(PASSES)]
+        s_codes = [keep.tile([P, SLOTS], U32, name=f"s_codes{s}", align_bytes=64) for s in range(PASSES)]
+        s_scales = [keep.tile([P, SLOTS], U8, name=f"s_scales{s}", align_bytes=64) for s in range(PASSES)]
+        w1_w = [keep.tile([P, E, 2 * H], U8, name=f"w1_w{s}", align_bytes=64) for s in range(PASSES)]
+        w1_s = keep.tile([P, PASSES, E, H], U8, name="w1_s", align_bytes=64)
+        w2_w = keep.tile([P, E, 2 * N], U8, name="w2_w", align_bytes=64)
+        w2_s = keep.tile([P, E, N], U8, name="w2_s", align_bytes=64)
+        y_out = keep.tile([P, N // P, RANKS, E, U], F32, name="y_out")
+        ident = keep.tile([P, P], F32, name="ident")
+
+        for s in range(PASSES):
+            nc.gpsimd.memset(t_scales[s][:].bitcast(I32), 0)
+        nc.vector.memset(w1_s[:].rearrange("p s e i -> p (s e i)").bitcast(I32), 0)
+        nc.vector.memset(w2_s[:].rearrange("p e n -> p (e n)").bitcast(I32), 0)
+        make_identity(nc, ident[:])
+
+        def load_x(s, a, b):
+            view = xT[512 * s : 512 * (s + 1), :].rearrange("(p j) t -> p j t", j=4)
+            nc.sync.dma_start(x_raw[s][:, :, a:b], view[:, :, a:b])
+
+        def load_w1(s, a, b):
+            nc.sync.dma_start(
+                w1_w[s][:, a:b, :].bitcast(I32),
+                w1_words[a:b, s].rearrange("e p b -> p e b").bitcast(I32),
+            )
+
+        def load_w1_scales(s):
+            view = w1_scales[:, s].rearrange("e (q r) i -> r q e i", r=4)
+            for r in range(4):
+                nc.sync.dma_start(w1_s[r:P:32, s, :, :].bitcast(I32), view[r].bitcast(I32))
+
+        def load_w2_scales():
+            view = w2_scales.rearrange("e s (q r) n -> r q (e s) n", r=4)
+            for r in range(4):
+                nc.sync.dma_start(w2_s[r:P:32, :, :].bitcast(I32), view[r].bitcast(I32))
+
+        load_x(0, 0, 256)
+        load_x(0, 256, 512)
+        load_x(0, 512, T)
+        nc.sync.dma_start(offsets[:], offs)
+        load_x(1, 0, T)
+        load_w1_scales(0)
+        load_x(2, 0, T)
+        load_w1(0, 0, E)
+        load_x(3, 0, T)
+        for s in (1, 2, 3):
+            load_w1_scales(s)
+        load_w1(1, 0, E)
+        load_w1(2, 0, E)
+        load_w2_scales()
+        nc.sync.dma_start(w2_w[:].bitcast(I32), w2_words.rearrange("e s p b -> p (e s) b").bitcast(I32))
+        for e in range(0, E, 2):
+            load_w1(3, e, e + 2)
+
+        def interleave(engine_copy, s, a, b):
+            engine_copy(
+                out=x_bf[s][:, a:b, :].rearrange("p (c i) j -> p c j i", i=4),
+                in_=x_raw[s][:, :, a:b].rearrange("p j (c i) -> p c j i", i=4),
+            )
+
+        def quantize_tokens(s, a, b):
+            nc.vector.quantize_mx(
+                out=t_codes[s][:, a:b].bitcast(FP8X4),
+                scales=t_scales[s][:, a:b],
+                in_=x_bf[s][:, a:b, :].rearrange("p t j -> p (t j)"),
+            )
+
+        def gather_codes(s, a, b):
+            entries = offsets[:, C * a // 16 : C * b // 16]
+            nc.vector.tensor_copy(s_codes[s][:, C * a : C * b], t_codes[s][:].indirect(entries))
+
+        def gather_scales(w, a, b):
+            entries = offsets[:, C * a // 16 : C * b // 16]
+            nc.vector.tensor_copy(s_scales[w][:, C * a : C * b], t_scales[w][:].indirect(entries))
+
+        acc = [psum.tile([P, H], F32, name=f"acc{e}", tag=f"bank{e}") for e in range(E)]
+
+        def layer1(s, e):
+            cols = slice(C * e, C * (e + 1))
+            nc.tensor.matmul_mx(
+                out=acc[e][:],
+                lhsT=s_codes[s][:, cols].bitcast(FP8X4),
+                lhsT_scale=s_scales[s][:, cols],
+                rhs=w1_w[s][:, e, :].bitcast(FP4X4),
+                rhs_scale=w1_s[:, s, e, :],
+                start=(s == 0),
+                stop=(s == PASSES - 1),
+            )
+
+        def hidden(e):
+            h = keep.tile([P, H], BF16, name=f"h{e}")
+            if e in VECTOR_RELU:
+                nc.vector.tensor_relu(h[:], acc[e][:])
+            else:
+                nc.scalar.activation(out=h[:], in_=acc[e][:], func=RELU)
+            words = h[:].bitcast(F32)
+            turned = psum.tile([P, 2, P], F32, name=f"turned{e}", tag=f"bank{6 if e == 0 else e - 1}")
+            for u in range(2):
+                nc.tensor.transpose(turned[:, u, :], words[:, u : 256 : 2], ident[:])
+            h_bf = keep.tile([P, C, 4], BF16, name=f"h_bf{e}", align_bytes=64)
+            nc.vector.tensor_copy(
+                out=h_bf[:].rearrange("p c j -> p (c j)").bitcast(F32).rearrange("p (c u) -> p c u", u=2),
+                in_=turned[:].rearrange("p u c -> p c u"),
+            )
+            return h_bf
+
+        def store(e0, e1):
+            for m in range(RANKS):
+                nc.sync.dma_start(
+                    out[:, 384 * m + U * e0 : 384 * m + U * e1].rearrange("(t p) c -> p t c", p=P),
+                    y_out[:, :, m, e0:e1, :].rearrange("p t e u -> p t (e u)"),
+                )
+
+        def layer2(e, h_bf):
+            h_codes = keep.tile([P, C], U32, name=f"h_codes{e}", align_bytes=64)
+            h_scales = keep.tile([P, C], U8, name=f"h_scales{e}", align_bytes=64)
+            nc.vector.quantize_mx(
+                out=h_codes[:].bitcast(FP8X4), scales=h_scales[:], in_=h_bf[:].rearrange("p c j -> p (c j)")
+            )
+            y = psum.tile([P, N // P, C], F32, name=f"y{e}", tag=f"bank{7 if e % 2 == 0 else 6}")
+            for t in range(N // P):
+                nc.tensor.matmul_mx(
+                    out=y[:, t, :],
+                    lhsT=w2_w[:, e, 2 * P * t : 2 * P * (t + 1)].bitcast(FP4X4),
+                    lhsT_scale=w2_s[:, e, P * t : P * (t + 1)],
+                    rhs=h_codes[:].bitcast(FP8X4),
+                    rhs_scale=h_scales[:],
+                    start=True,
+                    stop=True,
+                )
+            copy = nc.vector.tensor_copy if e in VECTOR_Y else nc.scalar.copy
+            copy(out=y_out[:, :, :, e, :], in_=y[:].rearrange("p t (m u) -> p t m u", m=RANKS))
+            if e in STORES:
+                store(STORES[e], e + 1)
+
+        HALVES = ((0, 3), (3, 6))
+        STORES = {1: 0, 3: 2, 4: 4, 5: 5}
+        VECTOR_RELU = (1, 3)
+        VECTOR_Y = (4,)
+        S, V = nc.scalar.copy, nc.vector.tensor_copy
+        MOVERS = ((S, V, S), (S, S, V), (S, S, S), (S, S, V))
+        for s in range(PASSES):
+            for mover, a, b in zip(MOVERS[s], (0, 256, 512), (256, 512, T)):
+                interleave(mover, s, a, b)
+            quantize_tokens(s, 0, 512)
+            quantize_tokens(s, 512, T)
+            if s < 3:
+                for a, b in HALVES:
+                    gather_codes(s, a, b)
+                    gather_scales(s, a, b)
+                for e in range(E):
+                    layer1(s, e)
+        for a in range(0, E, 2):
+            gather_codes(3, a, a + 2)
+            gather_scales(3, a, a + 2)
+            layer1(3, a)
+            layer1(3, a + 1)
+        waiting = hidden(0)
+        for e in range(E):
+            following = hidden(e + 1) if e + 1 < E else None
+            layer2(e, waiting)
+            waiting = following

@@ -21,75 +21,104 @@ FP8X4 = mybir.dt.float8_e4m3fn_x4
 FP4X4 = mybir.dt.float4_e2m1fn_x4
 RELU = mybir.ActivationFunctionType.Relu
 
+X_LOADS = (((0, 256), (256, 512), (512, T)), ((0, 256), (256, T)), ((0, T),), ((0, T),))
+X_MOVES = (
+    ((0, 256, "S"), (256, 512, "V"), (512, T, "S")),
+    ((0, 256, "S"), (256, T, "S")),
+    ((0, T, "S"),),
+    ((0, T, "S"),),
+)
+QUANT = ((0, 512), (512, T))
+HALVES = ((0, 3), (3, 6))
+HELD = 3
+W1_GROUPS = ((0, 3), (3, 6))
+W2_GROUPS = ((0, 3), (3, 6))
+SCALAR_Y = (1, 3, 4)
+TURN_GROUPS = ((0, 2, "S"), (2, 3, "S"), (3, 5, "V"), (5, 6, "S"))
+STORE_GROUPS = ((0, 3), (3, 5), (5, 6))
+
 
 def tile_moe_eps_mlp_relu_kernel(tc, xT, w1_words, w1_scales, w2_words, w2_scales, offs, out):
     nc = tc.nc
     with ExitStack() as ctx:
         keep = ctx.enter_context(tc.tile_pool(name="keep", bufs=1))
+        turns = ctx.enter_context(tc.tile_pool(name="turns", bufs=1))
         psum = ctx.enter_context(tc.psum_pool(name="psum", bufs=1))
 
         offsets = keep.tile([P, SLOTS // 16], U16, name="offsets")
-        x_raw = [keep.tile([P, 4, T], F32, name=f"x_raw{s}") for s in range(PASSES)]
-        x_bf = [keep.tile([P, T, 4], BF16, name=f"x_bf{s}", align_bytes=64) for s in range(PASSES)]
+        x_raw = {
+            (s, a): keep.tile([P, 4, b - a], F32, name=f"x_raw{s}_{a}") for s in range(PASSES) for a, b in X_LOADS[s]
+        }
+        x_bf = [keep.tile([P, T, 4], BF16, name=f"x_bf{s}", align_bytes=64) for s in range(PASSES - 1)]
+        x_bf.append(turns.tile([P, T, 4], BF16, name="x_bf_last", align_bytes=64, offset=0))
         t_codes = [keep.tile([P, T], U32, name=f"t_codes{s}", align_bytes=64) for s in range(PASSES)]
         t_scales = [keep.tile([P, T], U8, name=f"t_scales{s}", align_bytes=64) for s in range(PASSES)]
-        s_codes = [keep.tile([P, SLOTS], U32, name=f"s_codes{s}", align_bytes=64) for s in range(PASSES)]
-        s_scales = [keep.tile([P, SLOTS], U8, name=f"s_scales{s}", align_bytes=64) for s in range(PASSES)]
-        w1_w = [keep.tile([P, E, 2 * H], U8, name=f"w1_w{s}", align_bytes=64) for s in range(PASSES)]
-        w1_s = keep.tile([P, PASSES, E, H], U8, name="w1_s", align_bytes=64)
-        w2_w = keep.tile([P, E, 2 * N], U8, name="w2_w", align_bytes=64)
+        s_codes = {}
+        s_scales = {}
+        w1_w = {}
+        w1_s = {a: keep.tile([P, (b - a) * PASSES, H], U8, name=f"w1_s{a}", align_bytes=64) for a, b in W1_GROUPS}
+        w2_w = {a: keep.tile([P, b - a, 2 * N], U8, name=f"w2_w{a}", align_bytes=64) for a, b in W2_GROUPS}
         w2_s = keep.tile([P, E, N], U8, name="w2_s", align_bytes=64)
         y_out = keep.tile([P, N // P, RANKS, E, U], F32, name="y_out")
         ident = keep.tile([P, P], F32, name="ident")
 
         for s in range(PASSES):
             nc.gpsimd.memset(t_scales[s][:].bitcast(I32), 0)
-        nc.vector.memset(w1_s[:].rearrange("p s e i -> p (s e i)").bitcast(I32), 0)
-        nc.vector.memset(w2_s[:].rearrange("p e n -> p (e n)").bitcast(I32), 0)
         make_identity(nc, ident[:])
 
-        def load_x(s, a, b):
+        def load_x(s):
             view = xT[512 * s : 512 * (s + 1), :].rearrange("(p j) t -> p j t", j=4)
-            nc.sync.dma_start(x_raw[s][:, :, a:b], view[:, :, a:b])
+            for a, b in X_LOADS[s]:
+                nc.sync.dma_start(x_raw[s, a][:], view[:, :, a:b])
 
-        def load_w1(s, a, b):
+        def load_w1_passes(e, a, b):
+            if (e, a) == (E - 1, 0):
+                words = turns.tile([P, b - a, 2 * H], U8, name=f"w1_w{e}_{a}", align_bytes=64, offset=8 * T)
+            else:
+                words = keep.tile([P, b - a, 2 * H], U8, name=f"w1_w{e}_{a}", align_bytes=64)
+            nc.sync.dma_start(words[:].bitcast(I32), w1_words[e, a:b].rearrange("s p b -> p s b").bitcast(I32))
+            for s in range(a, b):
+                w1_w[e, s] = words[:, s - a, :]
+
+        def load_w1_experts(s, a, b):
+            words = keep.tile([P, b - a, 2 * H], U8, name=f"w1_w{a}_{s}", align_bytes=64)
+            nc.sync.dma_start(words[:].bitcast(I32), w1_words[a:b, s].rearrange("e p b -> p e b").bitcast(I32))
+            for e in range(a, b):
+                w1_w[e, s] = words[:, e - a, :]
+
+        def load_w2(a, b):
             nc.sync.dma_start(
-                w1_w[s][:, a:b, :].bitcast(I32),
-                w1_words[a:b, s].rearrange("e p b -> p e b").bitcast(I32),
+                w2_w[a][:].bitcast(I32), w2_words[a:b].rearrange("e s p b -> p (e s) b").bitcast(I32)
             )
 
-        def load_w1_scales(s):
-            view = w1_scales[:, s].rearrange("e (q r) i -> r q e i", r=4)
+        def load_scales(plane, scales):
+            view = scales.rearrange("e s (q r) i -> r q (e s) i", r=4)
             for r in range(4):
-                nc.sync.dma_start(w1_s[r:P:32, s, :, :].bitcast(I32), view[r].bitcast(I32))
+                nc.sync.dma_start(plane[r:P:32, :, :].bitcast(I32), view[r].bitcast(I32))
 
-        def load_w2_scales():
-            view = w2_scales.rearrange("e s (q r) n -> r q (e s) n", r=4)
-            for r in range(4):
-                nc.sync.dma_start(w2_s[r:P:32, :, :].bitcast(I32), view[r].bitcast(I32))
-
-        load_x(0, 0, 256)
-        load_x(0, 256, 512)
-        load_x(0, 512, T)
+        load_x(0)
         nc.sync.dma_start(offsets[:], offs)
-        load_x(1, 0, T)
-        load_w1_scales(0)
-        load_x(2, 0, T)
-        load_w1(0, 0, E)
-        load_x(3, 0, T)
-        for s in (1, 2, 3):
-            load_w1_scales(s)
-        load_w1(1, 0, E)
-        load_w1(2, 0, E)
-        load_w2_scales()
-        nc.sync.dma_start(w2_w[:].bitcast(I32), w2_words.rearrange("e s p b -> p (e s) b").bitcast(I32))
-        for e in range(0, E, 2):
-            load_w1(3, e, e + 2)
+        for s in range(1, PASSES):
+            load_x(s)
+        load_scales(w1_s[0], w1_scales[0:3])
+        for e in range(3):
+            load_w1_passes(e, 0, PASSES - 1)
+        load_w1_experts(PASSES - 1, 0, 3)
+        load_scales(w1_s[3], w1_scales[3:6])
+        load_w1_passes(3, 0, PASSES)
+        load_w1_passes(4, 0, PASSES)
+        load_w1_passes(5, 0, PASSES - 1)
+        load_w1_passes(5, PASSES - 1, PASSES)
+        load_scales(w2_s, w2_scales)
+        load_w2(0, 3)
+        load_w2(3, 6)
 
-        def interleave(engine_copy, s, a, b):
-            engine_copy(
+        def interleave(s, a, b, engine):
+            first = max(lo for lo, hi in X_LOADS[s] if lo <= a)
+            copy = nc.vector.tensor_copy if engine == "V" else nc.scalar.copy
+            copy(
                 out=x_bf[s][:, a:b, :].rearrange("p (c i) j -> p c j i", i=4),
-                in_=x_raw[s][:, :, a:b].rearrange("p j (c i) -> p c j i", i=4),
+                in_=x_raw[s, first][:, :, a - first : b - first].rearrange("p j (c i) -> p c j i", i=4),
             )
 
         def quantize_tokens(s, a, b):
@@ -99,98 +128,109 @@ def tile_moe_eps_mlp_relu_kernel(tc, xT, w1_words, w1_scales, w2_words, w2_scale
                 in_=x_bf[s][:, a:b, :].rearrange("p t j -> p (t j)"),
             )
 
-        def gather_codes(s, a, b):
+        def gather(s, a, b):
             entries = offsets[:, C * a // 16 : C * b // 16]
-            nc.vector.tensor_copy(s_codes[s][:, C * a : C * b], t_codes[s][:].indirect(entries))
-
-        def gather_scales(w, a, b):
-            entries = offsets[:, C * a // 16 : C * b // 16]
-            nc.vector.tensor_copy(s_scales[w][:, C * a : C * b], t_scales[w][:].indirect(entries))
+            width = C * (b - a)
+            if s == PASSES - 2 and a >= HELD:
+                place = 5 * C * (a - HELD)
+                codes = turns.tile([P, width], U32, name=f"s_codes{s}_{a}", align_bytes=64, offset=place)
+                scales = turns.tile([P, width], U8, name=f"s_scales{s}_{a}", align_bytes=64, offset=place + 4 * C)
+            else:
+                codes = keep.tile([P, width], U32, name=f"s_codes{s}_{a}", align_bytes=64)
+                scales = keep.tile([P, width], U8, name=f"s_scales{s}_{a}", align_bytes=64)
+            nc.vector.tensor_copy(codes[:], t_codes[s][:].indirect(entries))
+            nc.vector.tensor_copy(scales[:], t_scales[s][:].indirect(entries))
+            for e in range(a, b):
+                s_codes[s, e] = codes[:, C * (e - a) : C * (e - a + 1)]
+                s_scales[s, e] = scales[:, C * (e - a) : C * (e - a + 1)]
 
         acc = [psum.tile([P, H], F32, name=f"acc{e}", tag=f"bank{e}") for e in range(E)]
 
         def layer1(s, e):
-            cols = slice(C * e, C * (e + 1))
+            first = max(a for a, b in W1_GROUPS if a <= e)
             nc.tensor.matmul_mx(
                 out=acc[e][:],
-                lhsT=s_codes[s][:, cols].bitcast(FP8X4),
-                lhsT_scale=s_scales[s][:, cols],
-                rhs=w1_w[s][:, e, :].bitcast(FP4X4),
-                rhs_scale=w1_s[:, s, e, :],
+                lhsT=s_codes[s, e].bitcast(FP8X4),
+                lhsT_scale=s_scales[s, e],
+                rhs=w1_w[e, s].bitcast(FP4X4),
+                rhs_scale=w1_s[first][:, PASSES * (e - first) + s, :],
                 start=(s == 0),
                 stop=(s == PASSES - 1),
             )
 
-        def hidden(e):
-            h = keep.tile([P, H], BF16, name=f"h{e}")
-            if e in VECTOR_RELU:
-                nc.vector.tensor_relu(h[:], acc[e][:])
+        def relu(e):
+            if e == E - 2:
+                h = turns.tile([P, 2, P, 2], BF16, name=f"h{e}", align_bytes=64, offset=8 * T)
             else:
-                nc.scalar.activation(out=h[:], in_=acc[e][:], func=RELU)
-            words = h[:].bitcast(F32)
-            turned = psum.tile([P, 2, P], F32, name=f"turned{e}", tag=f"bank{6 if e == 0 else e - 1}")
-            for u in range(2):
-                nc.tensor.transpose(turned[:, u, :], words[:, u : 256 : 2], ident[:])
-            h_bf = keep.tile([P, C, 4], BF16, name=f"h_bf{e}", align_bytes=64)
-            nc.vector.tensor_copy(
+                h = keep.tile([P, 2, P, 2], BF16, name=f"h{e}")
+            nc.scalar.activation(out=h[:], in_=acc[e][:].rearrange("c (p u j) -> c u p j", u=2, j=2), func=RELU)
+            return h
+
+        def turn(a, b, engine, hidden):
+            width = C * (b - a)
+            turned = psum.tile([P, 2, width], F32, name=f"turned{a}", tag=f"bank{E + TURN_GROUPS.index((a, b, engine)) % 2}")
+            for e in range(a, b):
+                words = hidden[e - a][:].rearrange("c u p j -> c (u p j)").bitcast(F32)
+                for u in range(2):
+                    nc.tensor.transpose(
+                        turned[:, u, C * (e - a) : C * (e - a + 1)], words[:, P * u : P * (u + 1)], ident[:]
+                    )
+            h_bf = keep.tile([P, width, 4], BF16, name=f"h_bf{a}", align_bytes=64)
+            copy = nc.vector.tensor_copy if engine == "V" else nc.scalar.copy
+            copy(
                 out=h_bf[:].rearrange("p c j -> p (c j)").bitcast(F32).rearrange("p (c u) -> p c u", u=2),
                 in_=turned[:].rearrange("p u c -> p c u"),
             )
-            return h_bf
+            h_codes = keep.tile([P, width], U32, name=f"h_codes{a}", align_bytes=64)
+            h_scales = keep.tile([P, width], U8, name=f"h_scales{a}", align_bytes=64)
+            nc.vector.quantize_mx(
+                out=h_codes[:].bitcast(FP8X4), scales=h_scales[:], in_=h_bf[:].rearrange("p c j -> p (c j)")
+            )
+            return h_codes, h_scales
 
         def store(e0, e1):
             for m in range(RANKS):
                 nc.sync.dma_start(
-                    out[:, 384 * m + U * e0 : 384 * m + U * e1].rearrange("(t p) c -> p t c", p=P),
+                    out[:, E * U * m + U * e0 : E * U * m + U * e1].rearrange("(t p) c -> p t c", p=P),
                     y_out[:, :, m, e0:e1, :].rearrange("p t e u -> p t (e u)"),
                 )
 
-        def layer2(e, h_bf):
-            h_codes = keep.tile([P, C], U32, name=f"h_codes{e}", align_bytes=64)
-            h_scales = keep.tile([P, C], U8, name=f"h_scales{e}", align_bytes=64)
-            nc.vector.quantize_mx(
-                out=h_codes[:].bitcast(FP8X4), scales=h_scales[:], in_=h_bf[:].rearrange("p c j -> p (c j)")
-            )
-            y = psum.tile([P, N // P, C], F32, name=f"y{e}", tag=f"bank{7 if e % 2 == 0 else 6}")
+        def layer2(e, h_codes, h_scales):
+            first = max(a for a, b in W2_GROUPS if a <= e)
+            y = psum.tile([P, N // P, C], F32, name=f"y{e}", tag=f"bank{e}")
             for t in range(N // P):
                 nc.tensor.matmul_mx(
                     out=y[:, t, :],
-                    lhsT=w2_w[:, e, 2 * P * t : 2 * P * (t + 1)].bitcast(FP4X4),
+                    lhsT=w2_w[first][:, e - first, 2 * P * t : 2 * P * (t + 1)].bitcast(FP4X4),
                     lhsT_scale=w2_s[:, e, P * t : P * (t + 1)],
-                    rhs=h_codes[:].bitcast(FP8X4),
-                    rhs_scale=h_scales[:],
+                    rhs=h_codes.bitcast(FP8X4),
+                    rhs_scale=h_scales,
                     start=True,
                     stop=True,
                 )
-            copy = nc.vector.tensor_copy if e in VECTOR_Y else nc.scalar.copy
+            copy = nc.scalar.copy if e in SCALAR_Y else nc.vector.tensor_copy
             copy(out=y_out[:, :, :, e, :], in_=y[:].rearrange("p t (m u) -> p t m u", m=RANKS))
-            if e in STORES:
-                store(STORES[e], e + 1)
+            for a, b in STORE_GROUPS:
+                if e == b - 1:
+                    store(a, b)
 
-        HALVES = ((0, 3), (3, 6))
-        STORES = {1: 0, 3: 2, 4: 4, 5: 5}
-        VECTOR_RELU = (1, 3)
-        VECTOR_Y = (4,)
-        S, V = nc.scalar.copy, nc.vector.tensor_copy
-        MOVERS = ((S, V, S), (S, S, V), (S, S, S), (S, S, V))
         for s in range(PASSES):
-            for mover, a, b in zip(MOVERS[s], (0, 256, 512), (256, 512, T)):
-                interleave(mover, s, a, b)
-            quantize_tokens(s, 0, 512)
-            quantize_tokens(s, 512, T)
-            if s < 3:
-                for a, b in HALVES:
-                    gather_codes(s, a, b)
-                    gather_scales(s, a, b)
-                for e in range(E):
-                    layer1(s, e)
-        for a in range(0, E, 2):
-            gather_codes(3, a, a + 2)
-            gather_scales(3, a, a + 2)
-            layer1(3, a)
-            layer1(3, a + 1)
-        waiting = hidden(0)
+            for a, b, engine in X_MOVES[s]:
+                interleave(s, a, b, engine)
+            for a, b in QUANT:
+                quantize_tokens(s, a, b)
+            for a, b in HALVES[: max(0, min(2, PASSES - 1 - s))]:
+                gather(s, a, b)
         for e in range(E):
-            following = hidden(e + 1) if e + 1 < E else None
-            layer2(e, waiting)
-            waiting = following
+            for s in range(PASSES - 1 - e // 3, PASSES):
+                gather(s, e, e + 1)
+        for a, b, engine in TURN_GROUPS:
+            hidden = []
+            for e in range(a, b):
+                for s in range(PASSES):
+                    layer1(s, e)
+                hidden.append(relu(e))
+            h_codes, h_scales = turn(a, b, engine, hidden)
+            for e in range(a, b):
+                cols = slice(C * (e - a), C * (e - a + 1))
+                layer2(e, h_codes[:, cols], h_scales[:, cols])

@@ -31,10 +31,11 @@ X_MOVES = (
 QUANT = ((0, 512), (512, T))
 HALVES = ((0, 3), (3, 6))
 HELD = 3
+PASS_ORDER = (3, 2, 1, 0)
 W1_GROUPS = ((0, 3), (3, 6))
 W2_GROUPS = ((0, 3), (3, 6))
-SCALAR_Y = (1, 3, 4)
-TURN_GROUPS = ((0, 2, "S"), (2, 3, "S"), (3, 5, "V"), (5, 6, "S"))
+SCALAR_Y = (4,)
+TURN_GROUPS = ((0, 1, "S"), (1, 2, "S"), (2, 3, "S"), (3, 4, "S"), (4, 5, "V"), (5, 6, "S"))
 STORE_GROUPS = ((0, 3), (3, 5), (5, 6))
 
 
@@ -58,7 +59,7 @@ def tile_moe_eps_mlp_relu_kernel(tc, xT, w1_words, w1_scales, w2_words, w2_scale
         w1_w = {}
         w1_s = {a: keep.tile([P, (b - a) * PASSES, H], U8, name=f"w1_s{a}", align_bytes=64) for a, b in W1_GROUPS}
         w2_w = {a: keep.tile([P, b - a, 2 * N], U8, name=f"w2_w{a}", align_bytes=64) for a, b in W2_GROUPS}
-        w2_s = keep.tile([P, E, N], U8, name="w2_s", align_bytes=64)
+        w2_s = {a: keep.tile([P, b - a, N], U8, name=f"w2_s{a}", align_bytes=64) for a, b in W2_GROUPS}
         y_out = keep.tile([P, N // P, RANKS, E, U], F32, name="y_out")
         ident = keep.tile([P, P], F32, name="ident")
 
@@ -72,19 +73,10 @@ def tile_moe_eps_mlp_relu_kernel(tc, xT, w1_words, w1_scales, w2_words, w2_scale
                 nc.sync.dma_start(x_raw[s, a][:], view[:, :, a:b])
 
         def load_w1_passes(e, a, b):
-            if (e, a) == (E - 1, 0):
-                words = turns.tile([P, b - a, 2 * H], U8, name=f"w1_w{e}_{a}", align_bytes=64, offset=8 * T)
-            else:
-                words = keep.tile([P, b - a, 2 * H], U8, name=f"w1_w{e}_{a}", align_bytes=64)
+            words = keep.tile([P, b - a, 2 * H], U8, name=f"w1_w{e}_{a}", align_bytes=64)
             nc.sync.dma_start(words[:].bitcast(I32), w1_words[e, a:b].rearrange("s p b -> p s b").bitcast(I32))
             for s in range(a, b):
                 w1_w[e, s] = words[:, s - a, :]
-
-        def load_w1_experts(s, a, b):
-            words = keep.tile([P, b - a, 2 * H], U8, name=f"w1_w{a}_{s}", align_bytes=64)
-            nc.sync.dma_start(words[:].bitcast(I32), w1_words[a:b, s].rearrange("e p b -> p e b").bitcast(I32))
-            for e in range(a, b):
-                w1_w[e, s] = words[:, e - a, :]
 
         def load_w2(a, b):
             nc.sync.dma_start(
@@ -100,17 +92,17 @@ def tile_moe_eps_mlp_relu_kernel(tc, xT, w1_words, w1_scales, w2_words, w2_scale
         nc.sync.dma_start(offsets[:], offs)
         for s in range(1, PASSES):
             load_x(s)
-        load_scales(w1_s[0], w1_scales[0:3])
         for e in range(3):
-            load_w1_passes(e, 0, PASSES - 1)
-        load_w1_experts(PASSES - 1, 0, 3)
-        load_scales(w1_s[3], w1_scales[3:6])
+            load_w1_passes(e, 0, PASSES)
+        for a, b in W1_GROUPS:
+            load_scales(w1_s[a], w1_scales[a:b])
+        for a, b in W2_GROUPS:
+            load_scales(w2_s[a], w2_scales[a:b])
         load_w1_passes(3, 0, PASSES)
-        load_w1_passes(4, 0, PASSES)
-        load_w1_passes(5, 0, PASSES - 1)
-        load_w1_passes(5, PASSES - 1, PASSES)
-        load_scales(w2_s, w2_scales)
         load_w2(0, 3)
+        load_w1_passes(4, 0, PASSES)
+        load_w1_passes(5, 1, PASSES)
+        load_w1_passes(5, 0, 1)
         load_w2(3, 6)
 
         def interleave(s, a, b, engine):
@@ -135,6 +127,9 @@ def tile_moe_eps_mlp_relu_kernel(tc, xT, w1_words, w1_scales, w2_words, w2_scale
                 place = 5 * C * (a - HELD)
                 codes = turns.tile([P, width], U32, name=f"s_codes{s}_{a}", align_bytes=64, offset=place)
                 scales = turns.tile([P, width], U8, name=f"s_scales{s}_{a}", align_bytes=64, offset=place + 4 * C)
+            elif s == PASSES - 1:
+                codes = turns.tile([P, width], U32, name=f"s_codes{s}_{a}", align_bytes=64, offset=8 * T + 2 * H * a)
+                scales = keep.tile([P, width], U8, name=f"s_scales{s}_{a}", align_bytes=64)
             else:
                 codes = keep.tile([P, width], U32, name=f"s_codes{s}_{a}", align_bytes=64)
                 scales = keep.tile([P, width], U8, name=f"s_scales{s}_{a}", align_bytes=64)
@@ -154,13 +149,13 @@ def tile_moe_eps_mlp_relu_kernel(tc, xT, w1_words, w1_scales, w2_words, w2_scale
                 lhsT_scale=s_scales[s, e],
                 rhs=w1_w[e, s].bitcast(FP4X4),
                 rhs_scale=w1_s[first][:, PASSES * (e - first) + s, :],
-                start=(s == 0),
-                stop=(s == PASSES - 1),
+                start=(s == PASS_ORDER[0]),
+                stop=(s == PASS_ORDER[-1]),
             )
 
         def relu(e):
-            if e == E - 2:
-                h = turns.tile([P, 2, P, 2], BF16, name=f"h{e}", align_bytes=64, offset=8 * T)
+            if e < E - 1:
+                h = turns.tile([P, 2, P, 2], BF16, name=f"h{e}", align_bytes=64, offset=8 * T + 2 * H * (e + 1))
             else:
                 h = keep.tile([P, 2, P, 2], BF16, name=f"h{e}")
             nc.scalar.activation(out=h[:], in_=acc[e][:].rearrange("c (p u j) -> c u p j", u=2, j=2), func=RELU)
@@ -202,7 +197,7 @@ def tile_moe_eps_mlp_relu_kernel(tc, xT, w1_words, w1_scales, w2_words, w2_scale
                 nc.tensor.matmul_mx(
                     out=y[:, t, :],
                     lhsT=w2_w[first][:, e - first, 2 * P * t : 2 * P * (t + 1)].bitcast(FP4X4),
-                    lhsT_scale=w2_s[:, e, P * t : P * (t + 1)],
+                    lhsT_scale=w2_s[first][:, e - first, P * t : P * (t + 1)],
                     rhs=h_codes.bitcast(FP8X4),
                     rhs_scale=h_scales,
                     start=True,
@@ -224,13 +219,13 @@ def tile_moe_eps_mlp_relu_kernel(tc, xT, w1_words, w1_scales, w2_words, w2_scale
         for e in range(E):
             for s in range(PASSES - 1 - e // 3, PASSES):
                 gather(s, e, e + 1)
-        for a, b, engine in TURN_GROUPS:
-            hidden = []
-            for e in range(a, b):
-                for s in range(PASSES):
-                    layer1(s, e)
-                hidden.append(relu(e))
-            h_codes, h_scales = turn(a, b, engine, hidden)
-            for e in range(a, b):
-                cols = slice(C * (e - a), C * (e - a + 1))
-                layer2(e, h_codes[:, cols], h_scales[:, cols])
+        def finish(e):
+            h_codes, h_scales = turn(*TURN_GROUPS[e], [relu(e)])
+            layer2(e, h_codes[:], h_scales[:])
+
+        for e in range(E):
+            for s in PASS_ORDER:
+                layer1(s, e)
+            if e > 0:
+                finish(e - 1)
+        finish(E - 1)

@@ -31,11 +31,11 @@ X_MOVES = (
 QUANT = ((0, 512), (512, T))
 HALVES = ((0, 3), (3, 6))
 HELD = 3
-PASS_ORDER = (3, 2, 1, 0)
-W1_GROUPS = ((0, 3), (3, 6))
+PASS_ORDER = [(0, 1, 2, 3)] + [(3, 2, 1, 0)] * (E - 1)
+W1_GROUPS = ((0, 1), (1, 3), (3, 6))
 W2_GROUPS = ((0, 3), (3, 6))
-SCALAR_Y = (4,)
-TURN_GROUPS = ((0, 1, "S"), (1, 2, "S"), (2, 3, "S"), (3, 4, "S"), (4, 5, "V"), (5, 6, "S"))
+SCALAR_Y = (1, 4)
+TURN_GROUPS = ((0, 1, "S"), (1, 2, "S"), (2, 3, "S"), (3, 4, "S"), (4, 5, "S"), (5, 6, "S"))
 STORE_GROUPS = ((0, 3), (3, 5), (5, 6))
 
 
@@ -59,7 +59,7 @@ def tile_moe_eps_mlp_relu_kernel(tc, xT, w1_words, w1_scales, w2_words, w2_scale
         w1_w = {}
         w1_s = {a: keep.tile([P, (b - a) * PASSES, H], U8, name=f"w1_s{a}", align_bytes=64) for a, b in W1_GROUPS}
         w2_w = {a: keep.tile([P, b - a, 2 * N], U8, name=f"w2_w{a}", align_bytes=64) for a, b in W2_GROUPS}
-        w2_s = {a: keep.tile([P, b - a, N], U8, name=f"w2_s{a}", align_bytes=64) for a, b in W2_GROUPS}
+        w2_s = keep.tile([P, E, N], U8, name="w2_s", align_bytes=64)
         y_out = keep.tile([P, N // P, RANKS, E, U], F32, name="y_out")
         ident = keep.tile([P, P], F32, name="ident")
 
@@ -96,11 +96,10 @@ def tile_moe_eps_mlp_relu_kernel(tc, xT, w1_words, w1_scales, w2_words, w2_scale
             load_w1_passes(e, 0, PASSES)
         for a, b in W1_GROUPS:
             load_scales(w1_s[a], w1_scales[a:b])
-        for a, b in W2_GROUPS:
-            load_scales(w2_s[a], w2_scales[a:b])
+        load_scales(w2_s, w2_scales)
         load_w1_passes(3, 0, PASSES)
-        load_w2(0, 3)
         load_w1_passes(4, 0, PASSES)
+        load_w2(0, 3)
         load_w1_passes(5, 1, PASSES)
         load_w1_passes(5, 0, 1)
         load_w2(3, 6)
@@ -149,8 +148,8 @@ def tile_moe_eps_mlp_relu_kernel(tc, xT, w1_words, w1_scales, w2_words, w2_scale
                 lhsT_scale=s_scales[s, e],
                 rhs=w1_w[e, s].bitcast(FP4X4),
                 rhs_scale=w1_s[first][:, PASSES * (e - first) + s, :],
-                start=(s == PASS_ORDER[0]),
-                stop=(s == PASS_ORDER[-1]),
+                start=(s == PASS_ORDER[e][0]),
+                stop=(s == PASS_ORDER[e][-1]),
             )
 
         def relu(e):
@@ -197,7 +196,7 @@ def tile_moe_eps_mlp_relu_kernel(tc, xT, w1_words, w1_scales, w2_words, w2_scale
                 nc.tensor.matmul_mx(
                     out=y[:, t, :],
                     lhsT=w2_w[first][:, e - first, 2 * P * t : 2 * P * (t + 1)].bitcast(FP4X4),
-                    lhsT_scale=w2_s[first][:, e - first, P * t : P * (t + 1)],
+                    lhsT_scale=w2_s[:, e, P * t : P * (t + 1)],
                     rhs=h_codes.bitcast(FP8X4),
                     rhs_scale=h_scales,
                     start=True,
@@ -224,7 +223,7 @@ def tile_moe_eps_mlp_relu_kernel(tc, xT, w1_words, w1_scales, w2_words, w2_scale
             layer2(e, h_codes[:], h_scales[:])
 
         for e in range(E):
-            for s in PASS_ORDER:
+            for s in PASS_ORDER[e]:
                 layer1(s, e)
             if e > 0:
                 finish(e - 1)

@@ -21,21 +21,22 @@ FP8X4 = mybir.dt.float8_e4m3fn_x4
 FP4X4 = mybir.dt.float4_e2m1fn_x4
 RELU = mybir.ActivationFunctionType.Relu
 
-X_LOADS = (((0, 256), (256, 512), (512, T)), ((0, 256), (256, T)), ((0, T),), ((0, T),))
+X_LOADS = (((0, T),), ((0, T),), ((0, T),), ((0, T),))
 X_MOVES = (
-    ((0, 256, "S"), (256, 512, "V"), (512, T, "S")),
-    ((0, 256, "S"), (256, T, "S")),
+    ((0, 384, "V"), (384, T, "S")),
+    ((0, T, "S"),),
     ((0, T, "S"),),
     ((0, T, "S"),),
 )
 QUANT = ((0, 512), (512, T))
 HALVES = ((0, 3), (3, 6))
 HELD = 3
-PASS_ORDER = [(0, 1, 2, 3)] + [(3, 2, 1, 0)] * (E - 1)
+GATES = {(1, 0): 0, (3, 0): 2, (5, 0): 4}
+GATE_PLACE = {0: 8 * T, 2: 8 * T + 8 * H, 4: 8 * T + 12 * H}
 W1_GROUPS = ((0, 1), (1, 3), (3, 6))
 W2_GROUPS = ((0, 3), (3, 6))
 SCALAR_Y = (1, 4)
-TURN_GROUPS = ((0, 1, "S"), (1, 2, "S"), (2, 3, "S"), (3, 4, "S"), (4, 5, "S"), (5, 6, "S"))
+TURN_GROUPS = ((0, 1, "S"), (1, 2, "S"), (2, 3, "S"), (3, 4, "S"), (4, 5, "V"), (5, 6, "S"))
 STORE_GROUPS = ((0, 3), (3, 5), (5, 6))
 
 
@@ -73,7 +74,11 @@ def tile_moe_eps_mlp_relu_kernel(tc, xT, w1_words, w1_scales, w2_words, w2_scale
                 nc.sync.dma_start(x_raw[s, a][:], view[:, :, a:b])
 
         def load_w1_passes(e, a, b):
-            words = keep.tile([P, b - a, 2 * H], U8, name=f"w1_w{e}_{a}", align_bytes=64)
+            if (e, a) in GATES:
+                place = GATE_PLACE[GATES[e, a]]
+                words = turns.tile([P, b - a, 2 * H], U8, name=f"w1_w{e}_{a}", align_bytes=64, offset=place)
+            else:
+                words = keep.tile([P, b - a, 2 * H], U8, name=f"w1_w{e}_{a}", align_bytes=64)
             nc.sync.dma_start(words[:].bitcast(I32), w1_words[e, a:b].rearrange("s p b -> p s b").bitcast(I32))
             for s in range(a, b):
                 w1_w[e, s] = words[:, s - a, :]
@@ -97,11 +102,13 @@ def tile_moe_eps_mlp_relu_kernel(tc, xT, w1_words, w1_scales, w2_words, w2_scale
         for a, b in W1_GROUPS:
             load_scales(w1_s[a], w1_scales[a:b])
         load_scales(w2_s, w2_scales)
-        load_w1_passes(3, 0, PASSES)
+        load_w1_passes(3, 0, 2)
+        load_w1_passes(3, 2, PASSES)
         load_w1_passes(4, 0, PASSES)
         load_w2(0, 3)
-        load_w1_passes(5, 1, PASSES)
-        load_w1_passes(5, 0, 1)
+        load_w1_passes(5, 0, 2)
+        load_w1_passes(5, 2, 3)
+        load_w1_passes(5, 3, PASSES)
         load_w2(3, 6)
 
         def interleave(s, a, b, engine):
@@ -126,9 +133,6 @@ def tile_moe_eps_mlp_relu_kernel(tc, xT, w1_words, w1_scales, w2_words, w2_scale
                 place = 5 * C * (a - HELD)
                 codes = turns.tile([P, width], U32, name=f"s_codes{s}_{a}", align_bytes=64, offset=place)
                 scales = turns.tile([P, width], U8, name=f"s_scales{s}_{a}", align_bytes=64, offset=place + 4 * C)
-            elif s == PASSES - 1:
-                codes = turns.tile([P, width], U32, name=f"s_codes{s}_{a}", align_bytes=64, offset=8 * T + 2 * H * a)
-                scales = keep.tile([P, width], U8, name=f"s_scales{s}_{a}", align_bytes=64)
             else:
                 codes = keep.tile([P, width], U32, name=f"s_codes{s}_{a}", align_bytes=64)
                 scales = keep.tile([P, width], U8, name=f"s_scales{s}_{a}", align_bytes=64)
@@ -148,13 +152,13 @@ def tile_moe_eps_mlp_relu_kernel(tc, xT, w1_words, w1_scales, w2_words, w2_scale
                 lhsT_scale=s_scales[s, e],
                 rhs=w1_w[e, s].bitcast(FP4X4),
                 rhs_scale=w1_s[first][:, PASSES * (e - first) + s, :],
-                start=(s == PASS_ORDER[e][0]),
-                stop=(s == PASS_ORDER[e][-1]),
+                start=(s == 0),
+                stop=(s == PASSES - 1),
             )
 
         def relu(e):
-            if e < E - 1:
-                h = turns.tile([P, 2, P, 2], BF16, name=f"h{e}", align_bytes=64, offset=8 * T + 2 * H * (e + 1))
+            if e in GATE_PLACE:
+                h = turns.tile([P, 2, P, 2], BF16, name=f"h{e}", align_bytes=64, offset=GATE_PLACE[e])
             else:
                 h = keep.tile([P, 2, P, 2], BF16, name=f"h{e}")
             nc.scalar.activation(out=h[:], in_=acc[e][:].rearrange("c (p u j) -> c u p j", u=2, j=2), func=RELU)
@@ -218,13 +222,17 @@ def tile_moe_eps_mlp_relu_kernel(tc, xT, w1_words, w1_scales, w2_words, w2_scale
         for e in range(E):
             for s in range(PASSES - 1 - e // 3, PASSES):
                 gather(s, e, e + 1)
-        def finish(e):
-            h_codes, h_scales = turn(*TURN_GROUPS[e], [relu(e)])
-            layer2(e, h_codes[:], h_scales[:])
+
+        def finish(a, b, engine):
+            h_codes, h_scales = turn(a, b, engine, [relu(e) for e in range(a, b)])
+            for e in range(a, b):
+                cols = slice(C * (e - a), C * (e - a + 1))
+                layer2(e, h_codes[:, cols], h_scales[:, cols])
 
         for e in range(E):
-            for s in PASS_ORDER[e]:
+            for s in range(PASSES):
                 layer1(s, e)
-            if e > 0:
-                finish(e - 1)
-        finish(E - 1)
+            for a, b, engine in TURN_GROUPS:
+                if b == e:
+                    finish(a, b, engine)
+        finish(*TURN_GROUPS[-1])

@@ -6,9 +6,13 @@ from concourse.masks import make_identity
 K, T, E, C, H, N = 2048, 640, 6, 128, 512, 384
 RANKS = 2
 P = 128
-PASSES = K // 512
+PACK = 4
+PASSES = K // (P * PACK)
+LAST_PASS = PASSES - 1
+LAST_EXPERT = E - 1
 SLOTS = E * C
 U = C // RANKS
+N_TILES = N // P
 FLOPS = 2 * SLOTS * (K * H + H * N)
 
 F32 = mybir.dt.float32
@@ -21,23 +25,21 @@ FP8X4 = mybir.dt.float8_e4m3fn_x4
 FP4X4 = mybir.dt.float4_e2m1fn_x4
 RELU = mybir.ActivationFunctionType.Relu
 
-X_LOADS = (((0, T),), ((0, T),), ((0, T),), ((0, T),))
-X_MOVES = (
-    ((0, 384, "V"), (384, T, "S")),
-    ((0, T, "S"),),
-    ((0, T, "S"),),
-    ((0, T, "S"),),
-)
-QUANT = ((0, 512), (512, T))
+VECTOR_TOKENS = ((0, 384), (384, T), None, None)
+SCALAR_TOKENS = ((384, T), (0, 384), (0, T), (0, T))
+QUANTIZE_TOKENS = ((0, 512), (512, T))
 HALVES = ((0, 3), (3, 6))
-HELD = 3
-GATES = {(1, 0): 0, (3, 0): 2, (5, 0): 4}
-GATE_PLACE = {0: 8 * T, 2: 8 * T + 8 * H, 4: 8 * T + 12 * H}
-W1_GROUPS = ((0, 1), (1, 3), (3, 6))
-W2_GROUPS = ((0, 3), (3, 6))
-SCALAR_Y = (1, 4)
-TURN_GROUPS = ((0, 1, "S"), (1, 2, "S"), (2, 3, "S"), (3, 4, "S"), (4, 5, "V"), (5, 6, "S"))
-STORE_GROUPS = ((0, 3), (3, 5), (5, 6))
+EARLY = HALVES[0][1]
+LIVE_ROWS = 100
+W1_SCALE_GROUPS = ((0, 1), (1, 3), (3, 6))
+W2_PAIRS = ((0, 2), (2, 4), (4, 6))
+VECTOR_TURNS = (4,)
+SCALAR_Y = (0, 2)
+
+X_LAST_PLACE = 0
+X_LAST_BYTES = 2 * PACK * T
+PASS_BYTES = 2 * H
+H_PLACE = {0: X_LAST_BYTES, 2: X_LAST_BYTES + 4 * PASS_BYTES, 4: X_LAST_BYTES + 6 * PASS_BYTES}
 
 
 def tile_moe_eps_mlp_relu_kernel(tc, xT, w1_words, w1_scales, w2_words, w2_scales, offs, out):
@@ -47,192 +49,216 @@ def tile_moe_eps_mlp_relu_kernel(tc, xT, w1_words, w1_scales, w2_words, w2_scale
         turns = ctx.enter_context(tc.tile_pool(name="turns", bufs=1))
         psum = ctx.enter_context(tc.psum_pool(name="psum", bufs=1))
 
-        offsets = keep.tile([P, SLOTS // 16], U16, name="offsets")
-        x_raw = {
-            (s, a): keep.tile([P, 4, b - a], F32, name=f"x_raw{s}_{a}") for s in range(PASSES) for a, b in X_LOADS[s]
-        }
-        x_bf = [keep.tile([P, T, 4], BF16, name=f"x_bf{s}", align_bytes=64) for s in range(PASSES - 1)]
-        x_bf.append(turns.tile([P, T, 4], BF16, name="x_bf_last", align_bytes=64, offset=0))
-        t_codes = [keep.tile([P, T], U32, name=f"t_codes{s}", align_bytes=64) for s in range(PASSES)]
-        t_scales = [keep.tile([P, T], U8, name=f"t_scales{s}", align_bytes=64) for s in range(PASSES)]
-        s_codes = {}
-        s_scales = {}
-        w1_w = {}
-        w1_s = {a: keep.tile([P, (b - a) * PASSES, H], U8, name=f"w1_s{a}", align_bytes=64) for a, b in W1_GROUPS}
-        w2_w = {a: keep.tile([P, b - a, 2 * N], U8, name=f"w2_w{a}", align_bytes=64) for a, b in W2_GROUPS}
-        w2_s = keep.tile([P, E, N], U8, name="w2_s", align_bytes=64)
-        y_out = keep.tile([P, N // P, RANKS, E, U], F32, name="y_out")
-        ident = keep.tile([P, P], F32, name="ident")
+        def sbuf_tile(name, shape, dtype, place=None):
+            if place is None:
+                return keep.tile(shape, dtype, name=name, align_bytes=64)
+            return turns.tile(shape, dtype, name=name, align_bytes=64, offset=place)
 
-        for s in range(PASSES):
-            nc.gpsimd.memset(t_scales[s][:].bitcast(I32), 0)
+        offsets = keep.tile([P, SLOTS // 16], U16, name="offsets")
+        x_raw = [keep.tile([P, PACK, T], F32, name=f"x_raw{s}") for s in range(PASSES)]
+        x_bf = [
+            sbuf_tile(f"x_bf{s}", [P, T, PACK], BF16, X_LAST_PLACE if s == LAST_PASS else None) for s in range(PASSES)
+        ]
+        token_codes = [sbuf_tile(f"token_codes{s}", [P, T], U32) for s in range(PASSES)]
+        token_plane01 = sbuf_tile("token_plane01", [P, T], U8)
+        token_plane2 = sbuf_tile("token_plane2", [P, T], U8)
+        token_plane3 = sbuf_tile("token_plane3", [P, T], U8)
+        token_scales = [token_plane01[:], token_plane01[4:, :], token_plane2[:], token_plane3[:]]
+        slot_plane01 = sbuf_tile("slot_plane01", [P, SLOTS], U8)
+        slot_plane1 = sbuf_tile("slot_plane1", [P, SLOTS], U8)
+        w1_planes = {a: sbuf_tile(f"w1_planes{a}", [P, (b - a) * PASSES, H], U8) for a, b in W1_SCALE_GROUPS}
+        w2_planes = sbuf_tile("w2_planes", [P, E, N], U8)
+        y_out = keep.tile([P, N_TILES, RANKS, W2_PAIRS[-1][0], U], F32, name="y_out")
+        ident = keep.tile([P, P], F32, name="ident")
+        slot_codes, slot_scales, w1_codes, w2_codes = {}, {}, {}, {}
+
+        for plane in (token_plane01, token_plane2, token_plane3):
+            nc.gpsimd.memset(plane[:].bitcast(I32), 0)
         make_identity(nc, ident[:])
 
         def load_x(s):
-            view = xT[512 * s : 512 * (s + 1), :].rearrange("(p j) t -> p j t", j=4)
-            for a, b in X_LOADS[s]:
-                nc.sync.dma_start(x_raw[s, a][:], view[:, :, a:b])
+            rows = xT[P * PACK * s : P * PACK * (s + 1), :]
+            nc.sync.dma_start(x_raw[s][:], rows.rearrange("(p j) t -> p j t", j=PACK))
 
-        def load_w1_passes(e, a, b):
-            if (e, a) in GATES:
-                place = GATE_PLACE[GATES[e, a]]
-                words = turns.tile([P, b - a, 2 * H], U8, name=f"w1_w{e}_{a}", align_bytes=64, offset=place)
-            else:
-                words = keep.tile([P, b - a, 2 * H], U8, name=f"w1_w{e}_{a}", align_bytes=64)
+        def load_w1(e, a, b):
+            place = H_PLACE.get(e - 1) if a == 0 else None
+            words = sbuf_tile(f"w1_words{e}_{a}", [P, b - a, PASS_BYTES], U8, place)
             nc.sync.dma_start(words[:].bitcast(I32), w1_words[e, a:b].rearrange("s p b -> p s b").bitcast(I32))
             for s in range(a, b):
-                w1_w[e, s] = words[:, s - a, :]
+                w1_codes[e, s] = words[:, s - a, :]
 
         def load_w2(a, b):
-            nc.sync.dma_start(
-                w2_w[a][:].bitcast(I32), w2_words[a:b].rearrange("e s p b -> p (e s) b").bitcast(I32)
+            words = sbuf_tile(f"w2_words{a}", [P, b - a, 2 * N], U8)
+            nc.sync.dma_start(words[:].bitcast(I32), w2_words[a:b].rearrange("e s p b -> p (e s) b").bitcast(I32))
+            for e in range(a, b):
+                w2_codes[e] = words[:, e - a, :]
+
+        def load_scale_rows(planes, scales):
+            view = scales.rearrange("e s (g r) i -> r g (e s) i", r=4)
+            for r in range(4):
+                nc.sync.dma_start(planes[r:P:32, :, :].bitcast(I32), view[r].bitcast(I32))
+
+        def load_later_weights():
+            load_w1(EARLY - 1, 0, PASSES)
+            for a, b in W1_SCALE_GROUPS:
+                load_scale_rows(w1_planes[a], w1_scales[a:b])
+            load_scale_rows(w2_planes, w2_scales)
+            load_w1(3, 0, 2)
+            load_w1(3, 2, PASSES)
+            load_w2(*W2_PAIRS[0])
+            load_w1(4, 0, PASSES)
+            load_w2(*W2_PAIRS[1])
+            load_w1(LAST_EXPERT, 0, 2)
+            load_w1(LAST_EXPERT, 2, LAST_PASS)
+            load_w1(LAST_EXPERT, LAST_PASS, PASSES)
+            load_w2(*W2_PAIRS[2])
+
+        def interleave(copy, s, a, b):
+            copy(
+                out=x_bf[s][:, a:b, :].rearrange("p (c i) j -> p c j i", i=4),
+                in_=x_raw[s][:, :, a:b].rearrange("p j (c i) -> p c j i", i=4),
             )
 
-        def load_scales(plane, scales):
-            view = scales.rearrange("e s (q r) i -> r q (e s) i", r=4)
-            for r in range(4):
-                nc.sync.dma_start(plane[r:P:32, :, :].bitcast(I32), view[r].bitcast(I32))
+        def quantize_tokens(s):
+            if VECTOR_TOKENS[s]:
+                interleave(nc.vector.tensor_copy, s, *VECTOR_TOKENS[s])
+            interleave(nc.scalar.copy, s, *SCALAR_TOKENS[s])
+            for a, b in QUANTIZE_TOKENS:
+                nc.vector.quantize_mx(
+                    out=token_codes[s][:, a:b].bitcast(FP8X4),
+                    scales=token_scales[s][:, a:b],
+                    in_=x_bf[s][:, a:b, :].rearrange("p t j -> p (t j)"),
+                )
+
+        def entries(a, b):
+            return offsets[:, C * a // 16 : C * b // 16]
+
+        def gather_codes(s, a, b, place=None):
+            codes = sbuf_tile(f"slot_codes{s}_{a}", [P, C * (b - a)], U32, place)
+            nc.vector.tensor_copy(codes[:], token_codes[s][:].indirect(entries(a, b)))
+            for e in range(a, b):
+                slot_codes[e, s] = codes[:, C * (e - a) : C * (e - a + 1)]
+
+        def gather_scales(s, a, b, place=None):
+            scales = sbuf_tile(f"slot_scales{s}_{a}", [P, C * (b - a)], U8, place)
+            nc.vector.tensor_copy(scales[:], token_scales[s].indirect(entries(a, b)))
+            for e in range(a, b):
+                slot_scales[e, s] = scales[:, C * (e - a) : C * (e - a + 1)]
+
+        def gather_shared_plane():
+            for a, b in HALVES:
+                nc.vector.tensor_copy(slot_plane01[:, C * a : C * b], token_plane01[:].indirect(entries(a, b)))
+            nc.sync.dma_start(
+                slot_plane1[0:LIVE_ROWS, :].bitcast(I32), slot_plane01[4 : 4 + LIVE_ROWS, :].bitcast(I32)
+            )
+            for e in range(E):
+                slot_scales[e, 0] = slot_plane01[:, C * e : C * (e + 1)]
+                slot_scales[e, 1] = slot_plane1[:, C * e : C * (e + 1)]
+
+        acc = [psum.tile([P, H], F32, name=f"acc{e}", tag=f"bank{e}") for e in range(E)]
+
+        def first_layer(e):
+            first = max(a for a, b in W1_SCALE_GROUPS if a <= e)
+            for s in range(PASSES):
+                nc.tensor.matmul_mx(
+                    out=acc[e][:],
+                    lhsT=slot_codes[e, s].bitcast(FP8X4),
+                    lhsT_scale=slot_scales[e, s],
+                    rhs=w1_codes[e, s].bitcast(FP4X4),
+                    rhs_scale=w1_planes[first][:, PASSES * (e - first) + s, :],
+                    start=(s == 0),
+                    stop=(s == LAST_PASS),
+                )
+
+        def hidden(e):
+            h = sbuf_tile(f"h{e}", [P, 2, P, 2], BF16, H_PLACE.get(e))
+            nc.scalar.activation(out=h[:], in_=acc[e][:].rearrange("c (p u j) -> c u p j", u=2, j=2), func=RELU)
+            pairs = h[:].rearrange("c u p j -> c (u p j)").bitcast(F32)
+            turned = psum.tile([P, 2, C], F32, name=f"turned{e}", tag=f"bank{E + e % 2}")
+            for u in range(2):
+                nc.tensor.transpose(turned[:, u, :], pairs[:, P * u : P * (u + 1)], ident[:])
+            h_bf = sbuf_tile(f"h_bf{e}", [P, C * PACK], BF16)
+            copy = nc.vector.tensor_copy if e in VECTOR_TURNS else nc.scalar.copy
+            copy(
+                out=h_bf[:].bitcast(F32).rearrange("p (c u) -> p c u", u=2),
+                in_=turned[:].rearrange("p u c -> p c u"),
+            )
+            h_codes = sbuf_tile(f"h_codes{e}", [P, C], U32)
+            h_scales = sbuf_tile(f"h_scales{e}", [P, C], U8)
+            nc.vector.quantize_mx(out=h_codes[:].bitcast(FP8X4), scales=h_scales[:], in_=h_bf[:])
+            return h_codes, h_scales
+
+        def second_product(y, e, t, h_codes, h_scales):
+            nc.tensor.matmul_mx(
+                out=y,
+                lhsT=w2_codes[e][:, 2 * P * t : 2 * P * (t + 1)].bitcast(FP4X4),
+                lhsT_scale=w2_planes[:, e, P * t : P * (t + 1)],
+                rhs=h_codes[:].bitcast(FP8X4),
+                rhs_scale=h_scales[:],
+                start=True,
+                stop=True,
+            )
+
+        def second_layer(e):
+            h_codes, h_scales = hidden(e)
+            y = psum.tile([P, N_TILES, C], F32, name=f"y{e}", tag=f"bank{e}")
+            for t in range(N_TILES):
+                second_product(y[:, t, :], e, t, h_codes, h_scales)
+            copy = nc.scalar.copy if e in SCALAR_Y else nc.vector.tensor_copy
+            copy(out=y_out[:, :, :, e, :], in_=y[:].rearrange("p t (m u) -> p t m u", m=RANKS))
+
+        def store(a, b):
+            for m in range(RANKS):
+                nc.sync.dma_start(
+                    out[:, E * U * m + U * a : E * U * m + U * b].rearrange("(t p) c -> p t c", p=P),
+                    y_out[:, :, m, a:b, :].rearrange("p t e u -> p t (e u)"),
+                )
+
+        def last_second_layers(a, b):
+            h_mx = [hidden(e) for e in range(a, b)]
+            ys = [psum.tile([P, b - a, C], F32, name=f"y_last{t}", tag=f"bank{t}") for t in range(N_TILES)]
+            for e in range(a, b):
+                for t in range(N_TILES):
+                    second_product(ys[t][:, e - a, :], e, t, *h_mx[e - a])
+            for t in range(N_TILES):
+                rows = keep.tile([P, RANKS, b - a, U], F32, name=f"y_rows{t}")
+                copy = nc.scalar.copy if t % 2 else nc.vector.tensor_copy
+                copy(out=rows[:], in_=ys[t][:].rearrange("p e (m u) -> p m e u", m=RANKS))
+                view = out[P * t : P * (t + 1), :].rearrange("p (m c) -> p m c", m=RANKS)
+                nc.sync.dma_start(view[:, :, U * a : U * b], rows[:].rearrange("p m e u -> p m (e u)"))
 
         load_x(0)
         nc.sync.dma_start(offsets[:], offs)
         for s in range(1, PASSES):
             load_x(s)
-        for e in range(3):
-            load_w1_passes(e, 0, PASSES)
-        for a, b in W1_GROUPS:
-            load_scales(w1_s[a], w1_scales[a:b])
-        load_scales(w2_s, w2_scales)
-        load_w1_passes(3, 0, 2)
-        load_w1_passes(3, 2, PASSES)
-        load_w1_passes(4, 0, PASSES)
-        load_w2(0, 3)
-        load_w1_passes(5, 0, 2)
-        load_w1_passes(5, 2, 3)
-        load_w1_passes(5, 3, PASSES)
-        load_w2(3, 6)
+        for e in range(EARLY - 1):
+            load_w1(e, 0, PASSES)
 
-        def interleave(s, a, b, engine):
-            first = max(lo for lo, hi in X_LOADS[s] if lo <= a)
-            copy = nc.vector.tensor_copy if engine == "V" else nc.scalar.copy
-            copy(
-                out=x_bf[s][:, a:b, :].rearrange("p (c i) j -> p c j i", i=4),
-                in_=x_raw[s, first][:, :, a - first : b - first].rearrange("p j (c i) -> p c j i", i=4),
-            )
-
-        def quantize_tokens(s, a, b):
-            nc.vector.quantize_mx(
-                out=t_codes[s][:, a:b].bitcast(FP8X4),
-                scales=t_scales[s][:, a:b],
-                in_=x_bf[s][:, a:b, :].rearrange("p t j -> p (t j)"),
-            )
-
-        def gather(s, a, b):
-            entries = offsets[:, C * a // 16 : C * b // 16]
-            width = C * (b - a)
-            if s == PASSES - 2 and a >= HELD:
-                place = 5 * C * (a - HELD)
-                codes = turns.tile([P, width], U32, name=f"s_codes{s}_{a}", align_bytes=64, offset=place)
-                scales = turns.tile([P, width], U8, name=f"s_scales{s}_{a}", align_bytes=64, offset=place + 4 * C)
-            else:
-                codes = keep.tile([P, width], U32, name=f"s_codes{s}_{a}", align_bytes=64)
-                scales = keep.tile([P, width], U8, name=f"s_scales{s}_{a}", align_bytes=64)
-            nc.vector.tensor_copy(codes[:], t_codes[s][:].indirect(entries))
-            nc.vector.tensor_copy(scales[:], t_scales[s][:].indirect(entries))
-            for e in range(a, b):
-                s_codes[s, e] = codes[:, C * (e - a) : C * (e - a + 1)]
-                s_scales[s, e] = scales[:, C * (e - a) : C * (e - a + 1)]
-
-        acc = [psum.tile([P, H], F32, name=f"acc{e}", tag=f"bank{e}") for e in range(E)]
-
-        def layer1(s, e):
-            first = max(a for a, b in W1_GROUPS if a <= e)
-            nc.tensor.matmul_mx(
-                out=acc[e][:],
-                lhsT=s_codes[s, e].bitcast(FP8X4),
-                lhsT_scale=s_scales[s, e],
-                rhs=w1_w[e, s].bitcast(FP4X4),
-                rhs_scale=w1_s[first][:, PASSES * (e - first) + s, :],
-                start=(s == 0),
-                stop=(s == PASSES - 1),
-            )
-
-        def relu(e):
-            if e in GATE_PLACE:
-                h = turns.tile([P, 2, P, 2], BF16, name=f"h{e}", align_bytes=64, offset=GATE_PLACE[e])
-            else:
-                h = keep.tile([P, 2, P, 2], BF16, name=f"h{e}")
-            nc.scalar.activation(out=h[:], in_=acc[e][:].rearrange("c (p u j) -> c u p j", u=2, j=2), func=RELU)
-            return h
-
-        def turn(a, b, engine, hidden):
-            width = C * (b - a)
-            turned = psum.tile([P, 2, width], F32, name=f"turned{a}", tag=f"bank{E + TURN_GROUPS.index((a, b, engine)) % 2}")
-            for e in range(a, b):
-                words = hidden[e - a][:].rearrange("c u p j -> c (u p j)").bitcast(F32)
-                for u in range(2):
-                    nc.tensor.transpose(
-                        turned[:, u, C * (e - a) : C * (e - a + 1)], words[:, P * u : P * (u + 1)], ident[:]
-                    )
-            h_bf = keep.tile([P, width, 4], BF16, name=f"h_bf{a}", align_bytes=64)
-            copy = nc.vector.tensor_copy if engine == "V" else nc.scalar.copy
-            copy(
-                out=h_bf[:].rearrange("p c j -> p (c j)").bitcast(F32).rearrange("p (c u) -> p c u", u=2),
-                in_=turned[:].rearrange("p u c -> p c u"),
-            )
-            h_codes = keep.tile([P, width], U32, name=f"h_codes{a}", align_bytes=64)
-            h_scales = keep.tile([P, width], U8, name=f"h_scales{a}", align_bytes=64)
-            nc.vector.quantize_mx(
-                out=h_codes[:].bitcast(FP8X4), scales=h_scales[:], in_=h_bf[:].rearrange("p c j -> p (c j)")
-            )
-            return h_codes, h_scales
-
-        def store(e0, e1):
-            for m in range(RANKS):
-                nc.sync.dma_start(
-                    out[:, E * U * m + U * e0 : E * U * m + U * e1].rearrange("(t p) c -> p t c", p=P),
-                    y_out[:, :, m, e0:e1, :].rearrange("p t e u -> p t (e u)"),
-                )
-
-        def layer2(e, h_codes, h_scales):
-            first = max(a for a, b in W2_GROUPS if a <= e)
-            y = psum.tile([P, N // P, C], F32, name=f"y{e}", tag=f"bank{e}")
-            for t in range(N // P):
-                nc.tensor.matmul_mx(
-                    out=y[:, t, :],
-                    lhsT=w2_w[first][:, e - first, 2 * P * t : 2 * P * (t + 1)].bitcast(FP4X4),
-                    lhsT_scale=w2_s[:, e, P * t : P * (t + 1)],
-                    rhs=h_codes.bitcast(FP8X4),
-                    rhs_scale=h_scales,
-                    start=True,
-                    stop=True,
-                )
-            copy = nc.scalar.copy if e in SCALAR_Y else nc.vector.tensor_copy
-            copy(out=y_out[:, :, :, e, :], in_=y[:].rearrange("p t (m u) -> p t m u", m=RANKS))
-            for a, b in STORE_GROUPS:
-                if e == b - 1:
-                    store(a, b)
-
-        for s in range(PASSES):
-            for a, b, engine in X_MOVES[s]:
-                interleave(s, a, b, engine)
-            for a, b in QUANT:
-                quantize_tokens(s, a, b)
-            for a, b in HALVES[: max(0, min(2, PASSES - 1 - s))]:
-                gather(s, a, b)
+        quantize_tokens(0)
+        for a, b in HALVES:
+            gather_codes(0, a, b)
+        quantize_tokens(1)
+        gather_shared_plane()
+        load_later_weights()
+        for a, b in HALVES:
+            gather_codes(1, a, b)
+        quantize_tokens(2)
+        gather_codes(2, *HALVES[0])
+        gather_scales(2, *HALVES[0])
+        quantize_tokens(LAST_PASS)
         for e in range(E):
-            for s in range(PASSES - 1 - e // 3, PASSES):
-                gather(s, e, e + 1)
+            if e >= EARLY:
+                place = X_LAST_PLACE + 5 * C * (e - EARLY)
+                gather_codes(2, e, e + 1, place)
+                gather_scales(2, e, e + 1, place + 4 * C)
+            gather_codes(LAST_PASS, e, e + 1)
+            gather_scales(LAST_PASS, e, e + 1)
 
-        def finish(a, b, engine):
-            h_codes, h_scales = turn(a, b, engine, [relu(e) for e in range(a, b)])
-            for e in range(a, b):
-                cols = slice(C * (e - a), C * (e - a + 1))
-                layer2(e, h_codes[:, cols], h_scales[:, cols])
-
-        for e in range(E):
-            for s in range(PASSES):
-                layer1(s, e)
-            for a, b, engine in TURN_GROUPS:
-                if b == e:
-                    finish(a, b, engine)
-        finish(*TURN_GROUPS[-1])
+        last_pair = W2_PAIRS[-1]
+        first_layer(0)
+        for e in range(1, E):
+            first_layer(e)
+            if e <= last_pair[0]:
+                second_layer(e - 1)
+        store(0, last_pair[0])
+        last_second_layers(*last_pair)

@@ -33,13 +33,16 @@ EARLY = HALVES[0][1]
 LIVE_ROWS = 100
 W1_SCALE_GROUPS = ((0, 1), (1, 3), (3, 6))
 W2_PAIRS = ((0, 2), (2, 4), (4, 6))
+WARM_UPS = 4
 VECTOR_TURNS = (4,)
-SCALAR_Y = (0, 2)
+SCALAR_Y = (0, 3)
+TURNED_BANK = (1, 7, 6, 7, 6, 7)
 
 X_LAST_PLACE = 0
 X_LAST_BYTES = 2 * PACK * T
 PASS_BYTES = 2 * H
-H_PLACE = {0: X_LAST_BYTES, 2: X_LAST_BYTES + 4 * PASS_BYTES, 4: X_LAST_BYTES + 6 * PASS_BYTES}
+H_PLACE = {}
+TURNED_PLACE = {0: X_LAST_BYTES + 4 * PASS_BYTES, 1: X_LAST_BYTES + 5 * PASS_BYTES}
 
 
 def tile_moe_eps_mlp_relu_kernel(tc, xT, w1_words, w1_scales, w2_words, w2_scales, offs, out):
@@ -103,15 +106,13 @@ def tile_moe_eps_mlp_relu_kernel(tc, xT, w1_words, w1_scales, w2_words, w2_scale
             for a, b in W1_SCALE_GROUPS:
                 load_scale_rows(w1_planes[a], w1_scales[a:b])
             load_scale_rows(w2_planes, w2_scales)
-            load_w1(3, 0, 2)
-            load_w1(3, 2, PASSES)
-            load_w2(*W2_PAIRS[0])
-            load_w1(4, 0, PASSES)
-            load_w2(*W2_PAIRS[1])
-            load_w1(LAST_EXPERT, 0, 2)
-            load_w1(LAST_EXPERT, 2, LAST_PASS)
-            load_w1(LAST_EXPERT, LAST_PASS, PASSES)
-            load_w2(*W2_PAIRS[2])
+            for e in range(EARLY, E):
+                load_w1(e, 0, 2)
+                load_w1(e, 2, PASSES)
+                if e == EARLY:
+                    load_w2(*W2_PAIRS[0])
+            for a, b in W2_PAIRS[1:]:
+                load_w2(a, b)
 
         def interleave(copy, s, a, b):
             copy(
@@ -170,14 +171,27 @@ def tile_moe_eps_mlp_relu_kernel(tc, xT, w1_words, w1_scales, w2_words, w2_scale
                     stop=(s == LAST_PASS),
                 )
 
+        def warm_up():
+            unread = psum.tile([P, H], F32, name="unread", tag=f"bank{E + 1}")
+            for n in range(WARM_UPS):
+                nc.tensor.matmul_mx(
+                    out=unread[:],
+                    lhsT=slot_codes[0, 0].bitcast(FP8X4),
+                    lhsT_scale=slot_scales[0, 0],
+                    rhs=w1_codes[1, 0].bitcast(FP4X4),
+                    rhs_scale=slot_plane01[:, 0:H],
+                    start=True,
+                    stop=True,
+                )
+
         def hidden(e):
             h = sbuf_tile(f"h{e}", [P, 2, P, 2], BF16, H_PLACE.get(e))
             nc.scalar.activation(out=h[:], in_=acc[e][:].rearrange("c (p u j) -> c u p j", u=2, j=2), func=RELU)
             pairs = h[:].rearrange("c u p j -> c (u p j)").bitcast(F32)
-            turned = psum.tile([P, 2, C], F32, name=f"turned{e}", tag=f"bank{E + e % 2}")
+            turned = psum.tile([P, 2, C], F32, name=f"turned{e}", tag=f"bank{TURNED_BANK[e]}")
             for u in range(2):
                 nc.tensor.transpose(turned[:, u, :], pairs[:, P * u : P * (u + 1)], ident[:])
-            h_bf = sbuf_tile(f"h_bf{e}", [P, C * PACK], BF16)
+            h_bf = sbuf_tile(f"h_bf{e}", [P, C * PACK], BF16, TURNED_PLACE.get(e))
             copy = nc.vector.tensor_copy if e in VECTOR_TURNS else nc.scalar.copy
             copy(
                 out=h_bf[:].bitcast(F32).rearrange("p (c u) -> p c u", u=2),
@@ -199,8 +213,7 @@ def tile_moe_eps_mlp_relu_kernel(tc, xT, w1_words, w1_scales, w2_words, w2_scale
                 stop=True,
             )
 
-        def second_layer(e):
-            h_codes, h_scales = hidden(e)
+        def second_layer(e, h_codes, h_scales):
             y = psum.tile([P, N_TILES, C], F32, name=f"y{e}", tag=f"bank{e}")
             for t in range(N_TILES):
                 second_product(y[:, t, :], e, t, h_codes, h_scales)
@@ -216,7 +229,7 @@ def tile_moe_eps_mlp_relu_kernel(tc, xT, w1_words, w1_scales, w2_words, w2_scale
 
         def last_second_layers(a, b):
             h_mx = [hidden(e) for e in range(a, b)]
-            ys = [psum.tile([P, b - a, C], F32, name=f"y_last{t}", tag=f"bank{t}") for t in range(N_TILES)]
+            ys = [psum.tile([P, b - a, C], F32, name=f"y_last{t}", tag=f"bank{(0, 1, a)[t]}") for t in range(N_TILES)]
             for e in range(a, b):
                 for t in range(N_TILES):
                     second_product(ys[t][:, e - a, :], e, t, *h_mx[e - a])
@@ -240,25 +253,39 @@ def tile_moe_eps_mlp_relu_kernel(tc, xT, w1_words, w1_scales, w2_words, w2_scale
         quantize_tokens(1)
         gather_shared_plane()
         load_later_weights()
-        for a, b in HALVES:
-            gather_codes(1, a, b)
+        gather_codes(1, *HALVES[0])
         quantize_tokens(2)
         gather_codes(2, *HALVES[0])
         gather_scales(2, *HALVES[0])
         quantize_tokens(LAST_PASS)
-        for e in range(E):
+        for e in range(LAST_EXPERT):
             if e >= EARLY:
-                place = X_LAST_PLACE + 5 * C * (e - EARLY)
-                gather_codes(2, e, e + 1, place)
-                gather_scales(2, e, e + 1, place + 4 * C)
+                place = X_LAST_PLACE + 9 * C * (e - EARLY)
+                gather_codes(1, e, e + 1, place)
+                gather_codes(2, e, e + 1, place + 4 * C)
+                gather_scales(2, e, e + 1, place + 8 * C)
             gather_codes(LAST_PASS, e, e + 1)
             gather_scales(LAST_PASS, e, e + 1)
+        gather_codes(1, LAST_EXPERT, E, X_LAST_PLACE + 9 * C * (LAST_EXPERT - EARLY))
 
-        last_pair = W2_PAIRS[-1]
-        first_layer(0)
-        for e in range(1, E):
+        warm_up()
+        h_mx = []
+        for e in range(EARLY):
             first_layer(e)
-            if e <= last_pair[0]:
-                second_layer(e - 1)
-        store(0, last_pair[0])
-        last_second_layers(*last_pair)
+        for e in range(EARLY - 1):
+            h_mx.append(hidden(e))
+        for s in (2, LAST_PASS):
+            gather_codes(s, LAST_EXPERT, E, TURNED_PLACE[s - 2])
+            gather_scales(s, LAST_EXPERT, E, TURNED_PLACE[s - 2] + 4 * C)
+        h_mx.append(hidden(2))
+        first_layer(3)
+        for e in range(*W2_PAIRS[0]):
+            second_layer(e, *h_mx[e])
+        store(*W2_PAIRS[0])
+        first_layer(4)
+        h_mx.append(hidden(3))
+        first_layer(5)
+        for e in range(*W2_PAIRS[1]):
+            second_layer(e, *h_mx[e])
+        store(*W2_PAIRS[1])
+        last_second_layers(*W2_PAIRS[2])

@@ -30,19 +30,18 @@ SCALAR_TOKENS = ((384, T), (0, 384), (0, T), (0, T))
 QUANTIZE_TOKENS = ((0, 512), (512, T))
 HALVES = ((0, 3), (3, 6))
 EARLY = HALVES[0][1]
+FIRST = 2
 LIVE_ROWS = 100
-W1_SCALE_GROUPS = ((0, 1), (1, 3), (3, 6))
+W1_SCALE_GROUPS = ((0, 3), (3, 6))
 W2_PAIRS = ((0, 2), (2, 4), (4, 6))
-WARM_UPS = 4
 VECTOR_TURNS = (4,)
-SCALAR_Y = (0, 3)
-TURNED_BANK = (1, 7, 6, 7, 6, 7)
+SCALAR_Y = (0, 2)
+TURNED_BANK = {0: 1, 2: 3, 4: 6, 5: 7}
 
 X_LAST_PLACE = 0
 X_LAST_BYTES = 2 * PACK * T
 PASS_BYTES = 2 * H
-H_PLACE = {}
-TURNED_PLACE = {0: X_LAST_BYTES + 4 * PASS_BYTES, 1: X_LAST_BYTES + 5 * PASS_BYTES}
+TURNED_PLACE = X_LAST_BYTES
 
 
 def tile_moe_eps_mlp_relu_kernel(tc, xT, w1_words, w1_scales, w2_words, w2_scales, offs, out):
@@ -73,7 +72,7 @@ def tile_moe_eps_mlp_relu_kernel(tc, xT, w1_words, w1_scales, w2_words, w2_scale
         w2_planes = sbuf_tile("w2_planes", [P, E, N], U8)
         y_out = keep.tile([P, N_TILES, RANKS, W2_PAIRS[-1][0], U], F32, name="y_out")
         ident = keep.tile([P, P], F32, name="ident")
-        slot_codes, slot_scales, w1_codes, w2_codes = {}, {}, {}, {}
+        slot_codes, slot_scales, w1_codes, w2_codes, h_mx = {}, {}, {}, {}, {}
 
         for plane in (token_plane01, token_plane2, token_plane3):
             nc.gpsimd.memset(plane[:].bitcast(I32), 0)
@@ -84,11 +83,16 @@ def tile_moe_eps_mlp_relu_kernel(tc, xT, w1_words, w1_scales, w2_words, w2_scale
             nc.sync.dma_start(x_raw[s][:], rows.rearrange("(p j) t -> p j t", j=PACK))
 
         def load_w1(e, a, b):
-            place = H_PLACE.get(e - 1) if a == 0 else None
-            words = sbuf_tile(f"w1_words{e}_{a}", [P, b - a, PASS_BYTES], U8, place)
+            words = sbuf_tile(f"w1_words{e}_{a}", [P, b - a, PASS_BYTES], U8)
             nc.sync.dma_start(words[:].bitcast(I32), w1_words[e, a:b].rearrange("s p b -> p s b").bitcast(I32))
             for s in range(a, b):
                 w1_codes[e, s] = words[:, s - a, :]
+
+        def load_w1_pass(s):
+            words = sbuf_tile(f"w1_pass{s}", [P, FIRST, PASS_BYTES], U8)
+            nc.sync.dma_start(words[:].bitcast(I32), w1_words[0:FIRST, s].rearrange("e p b -> p e b").bitcast(I32))
+            for e in range(FIRST):
+                w1_codes[e, s] = words[:, e, :]
 
         def load_w2(a, b):
             words = sbuf_tile(f"w2_words{a}", [P, b - a, 2 * N], U8)
@@ -102,11 +106,12 @@ def tile_moe_eps_mlp_relu_kernel(tc, xT, w1_words, w1_scales, w2_words, w2_scale
                 nc.sync.dma_start(planes[r:P:32, :, :].bitcast(I32), view[r].bitcast(I32))
 
         def load_later_weights():
-            load_w1(EARLY - 1, 0, PASSES)
-            for a, b in W1_SCALE_GROUPS:
-                load_scale_rows(w1_planes[a], w1_scales[a:b])
-            load_scale_rows(w2_planes, w2_scales)
-            for e in range(EARLY, E):
+            for s in range(1, PASSES):
+                load_w1_pass(s)
+            for e in range(FIRST, E):
+                if e == EARLY:
+                    load_scale_rows(w1_planes[EARLY], w1_scales[EARLY:E])
+                    load_scale_rows(w2_planes, w2_scales)
                 load_w1(e, 0, 2)
                 load_w1(e, 2, PASSES)
                 if e == EARLY:
@@ -158,9 +163,9 @@ def tile_moe_eps_mlp_relu_kernel(tc, xT, w1_words, w1_scales, w2_words, w2_scale
 
         acc = [psum.tile([P, H], F32, name=f"acc{e}", tag=f"bank{e}") for e in range(E)]
 
-        def first_layer(e):
+        def first_layer(e, passes=range(PASSES)):
             first = max(a for a, b in W1_SCALE_GROUPS if a <= e)
-            for s in range(PASSES):
+            for s in passes:
                 nc.tensor.matmul_mx(
                     out=acc[e][:],
                     lhsT=slot_codes[e, s].bitcast(FP8X4),
@@ -171,44 +176,33 @@ def tile_moe_eps_mlp_relu_kernel(tc, xT, w1_words, w1_scales, w2_words, w2_scale
                     stop=(s == LAST_PASS),
                 )
 
-        def warm_up():
-            unread = psum.tile([P, H], F32, name="unread", tag=f"bank{E + 1}")
-            for n in range(WARM_UPS):
-                nc.tensor.matmul_mx(
-                    out=unread[:],
-                    lhsT=slot_codes[0, 0].bitcast(FP8X4),
-                    lhsT_scale=slot_scales[0, 0],
-                    rhs=w1_codes[1, 0].bitcast(FP4X4),
-                    rhs_scale=slot_plane01[:, 0:H],
-                    start=True,
-                    stop=True,
-                )
-
-        def hidden(e):
-            h = sbuf_tile(f"h{e}", [P, 2, P, 2], BF16, H_PLACE.get(e))
-            nc.scalar.activation(out=h[:], in_=acc[e][:].rearrange("c (p u j) -> c u p j", u=2, j=2), func=RELU)
-            pairs = h[:].rearrange("c u p j -> c (u p j)").bitcast(F32)
-            turned = psum.tile([P, 2, C], F32, name=f"turned{e}", tag=f"bank{TURNED_BANK[e]}")
-            for u in range(2):
-                nc.tensor.transpose(turned[:, u, :], pairs[:, P * u : P * (u + 1)], ident[:])
-            h_bf = sbuf_tile(f"h_bf{e}", [P, C * PACK], BF16, TURNED_PLACE.get(e))
-            copy = nc.vector.tensor_copy if e in VECTOR_TURNS else nc.scalar.copy
+        def hidden(a, b):
+            turned = psum.tile([P, b - a, 2, C], F32, name=f"turned{a}", tag=f"bank{TURNED_BANK[a]}")
+            for e in range(a, b):
+                h = sbuf_tile(f"h{e}", [P, 2, P, 2], BF16)
+                nc.scalar.activation(out=h[:], in_=acc[e][:].rearrange("c (p u j) -> c u p j", u=2, j=2), func=RELU)
+                pairs = h[:].rearrange("c u p j -> c (u p j)").bitcast(F32)
+                for u in range(2):
+                    nc.tensor.transpose(turned[:, e - a, u, :], pairs[:, P * u : P * (u + 1)], ident[:])
+            h_bf = sbuf_tile(f"h_bf{a}", [P, (b - a) * C * PACK], BF16, TURNED_PLACE if a == 0 else None)
+            copy = nc.vector.tensor_copy if a in VECTOR_TURNS else nc.scalar.copy
             copy(
-                out=h_bf[:].bitcast(F32).rearrange("p (c u) -> p c u", u=2),
-                in_=turned[:].rearrange("p u c -> p c u"),
+                out=h_bf[:].bitcast(F32).rearrange("p (e c u) -> p e c u", e=b - a, u=2),
+                in_=turned[:].rearrange("p e u c -> p e c u"),
             )
-            h_codes = sbuf_tile(f"h_codes{e}", [P, C], U32)
-            h_scales = sbuf_tile(f"h_scales{e}", [P, C], U8)
-            nc.vector.quantize_mx(out=h_codes[:].bitcast(FP8X4), scales=h_scales[:], in_=h_bf[:])
-            return h_codes, h_scales
+            codes = sbuf_tile(f"h_codes{a}", [P, (b - a) * C], U32)
+            scales = sbuf_tile(f"h_scales{a}", [P, (b - a) * C], U8)
+            nc.vector.quantize_mx(out=codes[:].bitcast(FP8X4), scales=scales[:], in_=h_bf[:])
+            for e in range(a, b):
+                h_mx[e] = codes[:, C * (e - a) : C * (e - a + 1)], scales[:, C * (e - a) : C * (e - a + 1)]
 
         def second_product(y, e, t, h_codes, h_scales):
             nc.tensor.matmul_mx(
                 out=y,
                 lhsT=w2_codes[e][:, 2 * P * t : 2 * P * (t + 1)].bitcast(FP4X4),
                 lhsT_scale=w2_planes[:, e, P * t : P * (t + 1)],
-                rhs=h_codes[:].bitcast(FP8X4),
-                rhs_scale=h_scales[:],
+                rhs=h_codes.bitcast(FP8X4),
+                rhs_scale=h_scales,
                 start=True,
                 stop=True,
             )
@@ -228,11 +222,12 @@ def tile_moe_eps_mlp_relu_kernel(tc, xT, w1_words, w1_scales, w2_words, w2_scale
                 )
 
         def last_second_layers(a, b):
-            h_mx = [hidden(e) for e in range(a, b)]
+            for e in range(a, b):
+                hidden(e, e + 1)
             ys = [psum.tile([P, b - a, C], F32, name=f"y_last{t}", tag=f"bank{(0, 1, a)[t]}") for t in range(N_TILES)]
             for e in range(a, b):
                 for t in range(N_TILES):
-                    second_product(ys[t][:, e - a, :], e, t, *h_mx[e - a])
+                    second_product(ys[t][:, e - a, :], e, t, *h_mx[e])
             for t in range(N_TILES):
                 rows = keep.tile([P, RANKS, b - a, U], F32, name=f"y_rows{t}")
                 copy = nc.scalar.copy if t % 2 else nc.vector.tensor_copy
@@ -244,8 +239,8 @@ def tile_moe_eps_mlp_relu_kernel(tc, xT, w1_words, w1_scales, w2_words, w2_scale
         nc.sync.dma_start(offsets[:], offs)
         for s in range(1, PASSES):
             load_x(s)
-        for e in range(EARLY - 1):
-            load_w1(e, 0, PASSES)
+        load_scale_rows(w1_planes[0], w1_scales[0:EARLY])
+        load_w1_pass(0)
 
         quantize_tokens(0)
         for a, b in HALVES:
@@ -264,26 +259,29 @@ def tile_moe_eps_mlp_relu_kernel(tc, xT, w1_words, w1_scales, w2_words, w2_scale
                 gather_codes(1, e, e + 1, place)
                 gather_codes(2, e, e + 1, place + 4 * C)
                 gather_scales(2, e, e + 1, place + 8 * C)
-            gather_codes(LAST_PASS, e, e + 1)
-            gather_scales(LAST_PASS, e, e + 1)
-        gather_codes(1, LAST_EXPERT, E, X_LAST_PLACE + 9 * C * (LAST_EXPERT - EARLY))
+            if e <= EARLY:
+                gather_codes(LAST_PASS, e, e + 1)
+                gather_scales(LAST_PASS, e, e + 1)
 
-        warm_up()
-        h_mx = []
-        for e in range(EARLY):
-            first_layer(e)
-        for e in range(EARLY - 1):
-            h_mx.append(hidden(e))
-        for s in (2, LAST_PASS):
-            gather_codes(s, LAST_EXPERT, E, TURNED_PLACE[s - 2])
-            gather_scales(s, LAST_EXPERT, E, TURNED_PLACE[s - 2] + 4 * C)
-        h_mx.append(hidden(2))
+        for s in range(PASSES):
+            for e in range(FIRST):
+                first_layer(e, (s,))
+        first_layer(2)
+        hidden(*W2_PAIRS[0])
+        place = TURNED_PLACE + 64 - 4 * C
+        gather_codes(LAST_PASS, 4, 5, place)
+        gather_scales(LAST_PASS, 4, 5, place + 4 * C)
+        gather_codes(1, 5, 6, place + 5 * C)
+        gather_codes(2, 5, 6, place + 9 * C)
+        gather_scales(2, 5, 6, place + 13 * C)
+        gather_codes(LAST_PASS, 5, 6, place + 14 * C)
+        gather_scales(LAST_PASS, 5, 6, place + 18 * C)
         first_layer(3)
         for e in range(*W2_PAIRS[0]):
             second_layer(e, *h_mx[e])
         store(*W2_PAIRS[0])
         first_layer(4)
-        h_mx.append(hidden(3))
+        hidden(*W2_PAIRS[1])
         first_layer(5)
         for e in range(*W2_PAIRS[1]):
             second_layer(e, *h_mx[e])

@@ -32,7 +32,8 @@ HALVES = ((0, 3), (3, 6))
 EARLY = HALVES[0][1]
 FIRST = 2
 LIVE_ROWS = 100
-W1_SCALE_GROUPS = ((0, 3), (3, 6))
+W1_SCALE_GROUPS = ((0, 4), (4, 6))
+SCALE_ROWS = 16
 W2_PAIRS = ((0, 2), (2, 4), (4, 6))
 VECTOR_TURNS = (4,)
 SCALAR_Y = (0, 2)
@@ -41,7 +42,8 @@ TURNED_BANK = {0: 1, 2: 3, 4: 6, 5: 7}
 X_LAST_PLACE = 0
 X_LAST_BYTES = 2 * PACK * T
 PASS_BYTES = 2 * H
-TURNED_PLACE = X_LAST_BYTES
+W_EARLY_BYTES = LAST_PASS * PASS_BYTES
+X2_PLACE = FIRST * W_EARLY_BYTES
 
 
 def tile_moe_eps_mlp_relu_kernel(tc, xT, w1_words, w1_scales, w2_words, w2_scales, offs, out):
@@ -59,7 +61,8 @@ def tile_moe_eps_mlp_relu_kernel(tc, xT, w1_words, w1_scales, w2_words, w2_scale
         offsets = keep.tile([P, SLOTS // 16], U16, name="offsets")
         x_raw = [keep.tile([P, PACK, T], F32, name=f"x_raw{s}") for s in range(PASSES)]
         x_bf = [
-            sbuf_tile(f"x_bf{s}", [P, T, PACK], BF16, X_LAST_PLACE if s == LAST_PASS else None) for s in range(PASSES)
+            sbuf_tile(f"x_bf{s}", [P, T, PACK], BF16, X2_PLACE if s == 2 else None)
+            for s in range(PASSES)
         ]
         token_codes = [sbuf_tile(f"token_codes{s}", [P, T], U32) for s in range(PASSES)]
         token_plane01 = sbuf_tile("token_plane01", [P, T], U8)
@@ -68,7 +71,10 @@ def tile_moe_eps_mlp_relu_kernel(tc, xT, w1_words, w1_scales, w2_words, w2_scale
         token_scales = [token_plane01[:], token_plane01[4:, :], token_plane2[:], token_plane3[:]]
         slot_plane01 = sbuf_tile("slot_plane01", [P, SLOTS], U8)
         slot_plane1 = sbuf_tile("slot_plane1", [P, SLOTS], U8)
-        w1_planes = {a: sbuf_tile(f"w1_planes{a}", [P, (b - a) * PASSES, H], U8) for a, b in W1_SCALE_GROUPS}
+        w1_planes = {
+            a: sbuf_tile(f"w1_planes{a}", [P, (b - a) * PASSES, H], U8, X2_PLACE if a else None)
+            for a, b in W1_SCALE_GROUPS
+        }
         w2_planes = sbuf_tile("w2_planes", [P, E, N], U8)
         y_out = keep.tile([P, N_TILES, RANKS, W2_PAIRS[-1][0], U], F32, name="y_out")
         ident = keep.tile([P, P], F32, name="ident")
@@ -82,17 +88,18 @@ def tile_moe_eps_mlp_relu_kernel(tc, xT, w1_words, w1_scales, w2_words, w2_scale
             rows = xT[P * PACK * s : P * PACK * (s + 1), :]
             nc.sync.dma_start(x_raw[s][:], rows.rearrange("(p j) t -> p j t", j=PACK))
 
-        def load_w1(e, a, b):
-            words = sbuf_tile(f"w1_words{e}_{a}", [P, b - a, PASS_BYTES], U8)
+        def load_w1(e, a, b, place=None):
+            words = sbuf_tile(f"w1_words{e}_{a}", [P, b - a, PASS_BYTES], U8, place)
             nc.sync.dma_start(words[:].bitcast(I32), w1_words[e, a:b].rearrange("s p b -> p s b").bitcast(I32))
             for s in range(a, b):
                 w1_codes[e, s] = words[:, s - a, :]
 
-        def load_w1_pass(s):
-            words = sbuf_tile(f"w1_pass{s}", [P, FIRST, PASS_BYTES], U8)
-            nc.sync.dma_start(words[:].bitcast(I32), w1_words[0:FIRST, s].rearrange("e p b -> p e b").bitcast(I32))
+        def load_w1_last_pass():
+            words = sbuf_tile("w1_last_pass", [P, FIRST, PASS_BYTES], U8)
+            view = w1_words[0:FIRST, LAST_PASS].rearrange("e p b -> p e b")
+            nc.sync.dma_start(words[:].bitcast(I32), view.bitcast(I32))
             for e in range(FIRST):
-                w1_codes[e, s] = words[:, e, :]
+                w1_codes[e, LAST_PASS] = words[:, e, :]
 
         def load_w2(a, b):
             words = sbuf_tile(f"w2_words{a}", [P, b - a, 2 * N], U8)
@@ -100,24 +107,16 @@ def tile_moe_eps_mlp_relu_kernel(tc, xT, w1_words, w1_scales, w2_words, w2_scale
             for e in range(a, b):
                 w2_codes[e] = words[:, e - a, :]
 
-        def load_scale_rows(planes, scales):
+        def load_scale_rows(queue, planes, scales):
             view = scales.rearrange("e s (g r) i -> r g (e s) i", r=4)
             for r in range(4):
-                nc.sync.dma_start(planes[r:P:32, :, :].bitcast(I32), view[r].bitcast(I32))
+                queue.dma_start(planes[r:P:32, :, :].bitcast(I32), view[r].bitcast(I32))
 
-        def load_later_weights():
-            for s in range(1, PASSES):
-                load_w1_pass(s)
-            for e in range(FIRST, E):
-                if e == EARLY:
-                    load_scale_rows(w1_planes[EARLY], w1_scales[EARLY:E])
-                    load_scale_rows(w2_planes, w2_scales)
-                load_w1(e, 0, 2)
-                load_w1(e, 2, PASSES)
-                if e == EARLY:
-                    load_w2(*W2_PAIRS[0])
-            for a, b in W2_PAIRS[1:]:
-                load_w2(a, b)
+        def load_early_scale_rows(run):
+            view = w1_scales[0 : W1_SCALE_GROUPS[0][1]].rearrange("e s q i -> q (e s) i")
+            for q in (2 * run, 8 + 2 * run, 2 * run + 1, 9 + 2 * run):
+                p = 32 * (q // 4) + q % 4
+                nc.sync.dma_start(w1_planes[0][p : p + 1, :, :].bitcast(I32), view[q : q + 1].bitcast(I32))
 
         def interleave(copy, s, a, b):
             copy(
@@ -154,7 +153,7 @@ def tile_moe_eps_mlp_relu_kernel(tc, xT, w1_words, w1_scales, w2_words, w2_scale
         def gather_shared_plane():
             for a, b in HALVES:
                 nc.vector.tensor_copy(slot_plane01[:, C * a : C * b], token_plane01[:].indirect(entries(a, b)))
-            nc.sync.dma_start(
+            nc.gpsimd.dma_start(
                 slot_plane1[0:LIVE_ROWS, :].bitcast(I32), slot_plane01[4 : 4 + LIVE_ROWS, :].bitcast(I32)
             )
             for e in range(E):
@@ -184,7 +183,7 @@ def tile_moe_eps_mlp_relu_kernel(tc, xT, w1_words, w1_scales, w2_words, w2_scale
                 pairs = h[:].rearrange("c u p j -> c (u p j)").bitcast(F32)
                 for u in range(2):
                     nc.tensor.transpose(turned[:, e - a, u, :], pairs[:, P * u : P * (u + 1)], ident[:])
-            h_bf = sbuf_tile(f"h_bf{a}", [P, (b - a) * C * PACK], BF16, TURNED_PLACE if a == 0 else None)
+            h_bf = sbuf_tile(f"h_bf{a}", [P, (b - a) * C * PACK], BF16)
             copy = nc.vector.tensor_copy if a in VECTOR_TURNS else nc.scalar.copy
             copy(
                 out=h_bf[:].bitcast(F32).rearrange("p (e c u) -> p e c u", e=b - a, u=2),
@@ -239,49 +238,54 @@ def tile_moe_eps_mlp_relu_kernel(tc, xT, w1_words, w1_scales, w2_words, w2_scale
         nc.sync.dma_start(offsets[:], offs)
         for s in range(1, PASSES):
             load_x(s)
-        load_scale_rows(w1_planes[0], w1_scales[0:EARLY])
-        load_w1_pass(0)
+            load_early_scale_rows(s - 1)
+        load_w1(0, 0, LAST_PASS, 0)
+        load_early_scale_rows(LAST_PASS)
+        load_w1(1, 0, LAST_PASS, W_EARLY_BYTES)
+        load_w1_last_pass()
+        for e in range(FIRST, LAST_EXPERT):
+            load_w1(e, 0, PASSES)
+            if e == 4:
+                load_scale_rows(nc.sync, w2_planes, w2_scales)
+                load_w2(*W2_PAIRS[0])
+        load_w1(LAST_EXPERT, 0, LAST_PASS)
+        load_w1(LAST_EXPERT, LAST_PASS, PASSES)
+        for a, b in W2_PAIRS[1:]:
+            load_w2(a, b)
 
         quantize_tokens(0)
         for a, b in HALVES:
             gather_codes(0, a, b)
         quantize_tokens(1)
         gather_shared_plane()
-        load_later_weights()
         gather_codes(1, *HALVES[0])
         quantize_tokens(2)
+        load_scale_rows(nc.gpsimd, w1_planes[W1_SCALE_GROUPS[1][0]], w1_scales[W1_SCALE_GROUPS[1][0] : E])
         gather_codes(2, *HALVES[0])
         gather_scales(2, *HALVES[0])
         quantize_tokens(LAST_PASS)
-        for e in range(LAST_EXPERT):
-            if e >= EARLY:
-                place = X_LAST_PLACE + 9 * C * (e - EARLY)
-                gather_codes(1, e, e + 1, place)
-                gather_codes(2, e, e + 1, place + 4 * C)
-                gather_scales(2, e, e + 1, place + 8 * C)
-            if e <= EARLY:
-                gather_codes(LAST_PASS, e, e + 1)
-                gather_scales(LAST_PASS, e, e + 1)
+        for a, b in ((0, FIRST), (FIRST, EARLY)):
+            gather_codes(LAST_PASS, a, b)
+            gather_scales(LAST_PASS, a, b)
 
-        for s in range(PASSES):
+        for passes in ((0, 2, 1), (LAST_PASS,)):
             for e in range(FIRST):
-                first_layer(e, (s,))
+                first_layer(e, passes)
+        for e in range(EARLY, E):
+            place = 14 * C * (e - EARLY)
+            gather_codes(1, e, e + 1, place)
+            gather_codes(2, e, e + 1, place + 4 * C)
+            gather_scales(2, e, e + 1, place + 8 * C)
+            gather_codes(LAST_PASS, e, e + 1, place + 9 * C)
+            gather_scales(LAST_PASS, e, e + 1, place + 13 * C)
         first_layer(2)
         hidden(*W2_PAIRS[0])
-        place = TURNED_PLACE + 64 - 4 * C
-        gather_codes(LAST_PASS, 4, 5, place)
-        gather_scales(LAST_PASS, 4, 5, place + 4 * C)
-        gather_codes(1, 5, 6, place + 5 * C)
-        gather_codes(2, 5, 6, place + 9 * C)
-        gather_scales(2, 5, 6, place + 13 * C)
-        gather_codes(LAST_PASS, 5, 6, place + 14 * C)
-        gather_scales(LAST_PASS, 5, 6, place + 18 * C)
         first_layer(3)
+        first_layer(4)
+        hidden(*W2_PAIRS[1])
         for e in range(*W2_PAIRS[0]):
             second_layer(e, *h_mx[e])
         store(*W2_PAIRS[0])
-        first_layer(4)
-        hidden(*W2_PAIRS[1])
         first_layer(5)
         for e in range(*W2_PAIRS[1]):
             second_layer(e, *h_mx[e])

@@ -26,7 +26,7 @@ FP4X4 = mybir.dt.float4_e2m1fn_x4
 RELU = mybir.ActivationFunctionType.Relu
 
 VECTOR_TOKENS = ((0, 384), (384, T), None, None)
-SCALAR_TOKENS = ((384, T), (0, 384), (0, T), (0, T))
+SCALAR_TOKENS = (((384, T),), ((0, 384),), ((0, 512), (512, T)), ((0, 512), (512, T)))
 QUANTIZE_TOKENS = ((0, 512), (512, T))
 HALVES = ((0, 3), (3, 6))
 EARLY = HALVES[0][1]
@@ -61,7 +61,7 @@ def tile_moe_eps_mlp_relu_kernel(tc, xT, w1_words, w1_scales, w2_words, w2_scale
         offsets = keep.tile([P, SLOTS // 16], U16, name="offsets")
         x_raw = [keep.tile([P, PACK, T], F32, name=f"x_raw{s}") for s in range(PASSES)]
         x_bf = [
-            sbuf_tile(f"x_bf{s}", [P, T, PACK], BF16, X2_PLACE if s == 2 else None)
+            sbuf_tile(f"x_bf{s}", [P, T, PACK], BF16, None)
             for s in range(PASSES)
         ]
         token_codes = [sbuf_tile(f"token_codes{s}", [P, T], U32) for s in range(PASSES)]
@@ -72,7 +72,7 @@ def tile_moe_eps_mlp_relu_kernel(tc, xT, w1_words, w1_scales, w2_words, w2_scale
         slot_plane01 = sbuf_tile("slot_plane01", [P, SLOTS], U8)
         slot_plane1 = sbuf_tile("slot_plane1", [P, SLOTS], U8)
         w1_planes = {
-            a: sbuf_tile(f"w1_planes{a}", [P, (b - a) * PASSES, H], U8, X2_PLACE if a else None)
+            a: sbuf_tile(f"w1_planes{a}", [P, (b - a) * PASSES, H], U8)
             for a, b in W1_SCALE_GROUPS
         }
         w2_planes = sbuf_tile("w2_planes", [P, E, N], U8)
@@ -94,12 +94,12 @@ def tile_moe_eps_mlp_relu_kernel(tc, xT, w1_words, w1_scales, w2_words, w2_scale
             for s in range(a, b):
                 w1_codes[e, s] = words[:, s - a, :]
 
-        def load_w1_last_pass():
-            words = sbuf_tile("w1_last_pass", [P, FIRST, PASS_BYTES], U8)
-            view = w1_words[0:FIRST, LAST_PASS].rearrange("e p b -> p e b")
-            nc.sync.dma_start(words[:].bitcast(I32), view.bitcast(I32))
+        def load_w1_pass(s):
+            place = FIRST * PASS_BYTES * s if s < 2 else None
+            words = sbuf_tile(f"w1_pass{s}", [P, FIRST, PASS_BYTES], U8, place)
+            nc.sync.dma_start(words[:].bitcast(I32), w1_words[0:FIRST, s].rearrange("e p b -> p e b").bitcast(I32))
             for e in range(FIRST):
-                w1_codes[e, LAST_PASS] = words[:, e, :]
+                w1_codes[e, s] = words[:, e, :]
 
         def load_w2(a, b):
             words = sbuf_tile(f"w2_words{a}", [P, b - a, 2 * N], U8)
@@ -112,9 +112,10 @@ def tile_moe_eps_mlp_relu_kernel(tc, xT, w1_words, w1_scales, w2_words, w2_scale
             for r in range(4):
                 queue.dma_start(planes[r:P:32, :, :].bitcast(I32), view[r].bitcast(I32))
 
-        def load_early_scale_rows(run):
+        def load_early_scale_rows(a, b):
             view = w1_scales[0 : W1_SCALE_GROUPS[0][1]].rearrange("e s q i -> q (e s) i")
-            for q in (2 * run, 8 + 2 * run, 2 * run + 1, 9 + 2 * run):
+            for n in range(a, b):
+                q = n // 2 + SCALE_ROWS // 2 * (n % 2)
                 p = 32 * (q // 4) + q % 4
                 nc.sync.dma_start(w1_planes[0][p : p + 1, :, :].bitcast(I32), view[q : q + 1].bitcast(I32))
 
@@ -127,7 +128,8 @@ def tile_moe_eps_mlp_relu_kernel(tc, xT, w1_words, w1_scales, w2_words, w2_scale
         def quantize_tokens(s):
             if VECTOR_TOKENS[s]:
                 interleave(nc.vector.tensor_copy, s, *VECTOR_TOKENS[s])
-            interleave(nc.scalar.copy, s, *SCALAR_TOKENS[s])
+            for a, b in SCALAR_TOKENS[s]:
+                interleave(nc.scalar.copy, s, a, b)
             for a, b in QUANTIZE_TOKENS:
                 nc.vector.quantize_mx(
                     out=token_codes[s][:, a:b].bitcast(FP8X4),
@@ -150,10 +152,17 @@ def tile_moe_eps_mlp_relu_kernel(tc, xT, w1_words, w1_scales, w2_words, w2_scale
             for e in range(a, b):
                 slot_scales[e, s] = scales[:, C * (e - a) : C * (e - a + 1)]
 
+        def gather_late(e, place):
+            gather_codes(1, e, e + 1, place)
+            gather_codes(2, e, e + 1, place + 4 * C)
+            gather_scales(2, e, e + 1, place + 8 * C)
+            gather_codes(LAST_PASS, e, e + 1, place + 9 * C)
+            gather_scales(LAST_PASS, e, e + 1, place + 13 * C)
+
         def gather_shared_plane():
             for a, b in HALVES:
                 nc.vector.tensor_copy(slot_plane01[:, C * a : C * b], token_plane01[:].indirect(entries(a, b)))
-            nc.gpsimd.dma_start(
+            nc.sync.dma_start(
                 slot_plane1[0:LIVE_ROWS, :].bitcast(I32), slot_plane01[4 : 4 + LIVE_ROWS, :].bitcast(I32)
             )
             for e in range(E):
@@ -183,7 +192,7 @@ def tile_moe_eps_mlp_relu_kernel(tc, xT, w1_words, w1_scales, w2_words, w2_scale
                 pairs = h[:].rearrange("c u p j -> c (u p j)").bitcast(F32)
                 for u in range(2):
                     nc.tensor.transpose(turned[:, e - a, u, :], pairs[:, P * u : P * (u + 1)], ident[:])
-            h_bf = sbuf_tile(f"h_bf{a}", [P, (b - a) * C * PACK], BF16)
+            h_bf = sbuf_tile(f"h_bf{a}", [P, (b - a) * C * PACK], BF16, X2_PLACE if a == 0 else None)
             copy = nc.vector.tensor_copy if a in VECTOR_TURNS else nc.scalar.copy
             copy(
                 out=h_bf[:].bitcast(F32).rearrange("p (e c u) -> p e c u", e=b - a, u=2),
@@ -238,29 +247,29 @@ def tile_moe_eps_mlp_relu_kernel(tc, xT, w1_words, w1_scales, w2_words, w2_scale
         nc.sync.dma_start(offsets[:], offs)
         for s in range(1, PASSES):
             load_x(s)
-            load_early_scale_rows(s - 1)
-        load_w1(0, 0, LAST_PASS, 0)
-        load_early_scale_rows(LAST_PASS)
-        load_w1(1, 0, LAST_PASS, W_EARLY_BYTES)
-        load_w1_last_pass()
-        for e in range(FIRST, LAST_EXPERT):
-            load_w1(e, 0, PASSES)
-            if e == 4:
-                load_scale_rows(nc.sync, w2_planes, w2_scales)
-                load_w2(*W2_PAIRS[0])
-        load_w1(LAST_EXPERT, 0, LAST_PASS)
-        load_w1(LAST_EXPERT, LAST_PASS, PASSES)
-        for a, b in W2_PAIRS[1:]:
-            load_w2(a, b)
+            load_early_scale_rows(6 * (s - 1), min(6 * s, SCALE_ROWS))
+        load_w1_pass(0)
 
         quantize_tokens(0)
         for a, b in HALVES:
             gather_codes(0, a, b)
         quantize_tokens(1)
         gather_shared_plane()
+        for s in range(1, PASSES):
+            load_w1_pass(s)
+        for e in range(FIRST, LAST_EXPERT):
+            load_w1(e, 0, PASSES)
+            if e == 2:
+                load_scale_rows(nc.sync, w1_planes[W1_SCALE_GROUPS[1][0]], w1_scales[W1_SCALE_GROUPS[1][0] : E])
+                load_scale_rows(nc.sync, w2_planes, w2_scales)
+            if e == 4:
+                load_w2(*W2_PAIRS[0])
+        load_w1(LAST_EXPERT, 0, LAST_PASS)
+        load_w1(LAST_EXPERT, LAST_PASS, PASSES)
+        for a, b in W2_PAIRS[1:]:
+            load_w2(a, b)
         gather_codes(1, *HALVES[0])
         quantize_tokens(2)
-        load_scale_rows(nc.gpsimd, w1_planes[W1_SCALE_GROUPS[1][0]], w1_scales[W1_SCALE_GROUPS[1][0] : E])
         gather_codes(2, *HALVES[0])
         gather_scales(2, *HALVES[0])
         quantize_tokens(LAST_PASS)
@@ -268,18 +277,14 @@ def tile_moe_eps_mlp_relu_kernel(tc, xT, w1_words, w1_scales, w2_words, w2_scale
             gather_codes(LAST_PASS, a, b)
             gather_scales(LAST_PASS, a, b)
 
-        for passes in ((0, 2, 1), (LAST_PASS,)):
+        for s in range(PASSES):
             for e in range(FIRST):
-                first_layer(e, passes)
-        for e in range(EARLY, E):
-            place = 14 * C * (e - EARLY)
-            gather_codes(1, e, e + 1, place)
-            gather_codes(2, e, e + 1, place + 4 * C)
-            gather_scales(2, e, e + 1, place + 8 * C)
-            gather_codes(LAST_PASS, e, e + 1, place + 9 * C)
-            gather_scales(LAST_PASS, e, e + 1, place + 13 * C)
+                first_layer(e, (s,))
+        for e in range(EARLY, LAST_EXPERT):
+            gather_late(e, 14 * C * (e - EARLY))
         first_layer(2)
         hidden(*W2_PAIRS[0])
+        gather_late(LAST_EXPERT, X2_PLACE)
         first_layer(3)
         first_layer(4)
         hidden(*W2_PAIRS[1])

@@ -29,21 +29,23 @@ VECTOR_TOKENS = ((0, 384), (384, T), None, None)
 SCALAR_TOKENS = (((384, T),), ((0, 384),), ((0, 512), (512, T)), ((0, 512), (512, T)))
 QUANTIZE_TOKENS = ((0, 512), (512, T))
 HALVES = ((0, 3), (3, 6))
-EARLY = HALVES[0][1]
-FIRST = 2
 LIVE_ROWS = 100
-W1_SCALE_GROUPS = ((0, 4), (4, 6))
-SCALE_ROWS = 16
-W2_PAIRS = ((0, 2), (2, 4), (4, 6))
+FIRST = 2
+PAIRS = ((0, 2), (2, 4), (4, 6))
+PASS_BYTES = 2 * H
+X_LAST_PLACE = 0
+X_BYTES = 2 * PACK * T
+X2_PLACE = X_BYTES
+TURNED_PLACE = 2 * X_BYTES
+RAW_BYTES = 4 * PACK * T
+RAW2_PLACE = TURNED_PLACE + 2 * PASS_BYTES
+RAW_PLACES = (None, None, RAW2_PLACE, None)
+W2_PLANES_PLACE = RAW2_PLACE + 2 * PASSES * H
+X_PLACES = (None, None, X2_PLACE, X_LAST_PLACE)
+EARLY = 4
 VECTOR_TURNS = (4,)
 SCALAR_Y = (0, 2)
 TURNED_BANK = {0: 1, 2: 3, 4: 6, 5: 7}
-
-X_LAST_PLACE = 0
-X_LAST_BYTES = 2 * PACK * T
-PASS_BYTES = 2 * H
-W_EARLY_BYTES = LAST_PASS * PASS_BYTES
-X2_PLACE = FIRST * W_EARLY_BYTES
 
 
 def tile_moe_eps_mlp_relu_kernel(tc, xT, w1_words, w1_scales, w2_words, w2_scales, offs, out):
@@ -59,28 +61,18 @@ def tile_moe_eps_mlp_relu_kernel(tc, xT, w1_words, w1_scales, w2_words, w2_scale
             return turns.tile(shape, dtype, name=name, align_bytes=64, offset=place)
 
         offsets = keep.tile([P, SLOTS // 16], U16, name="offsets")
-        x_raw = [keep.tile([P, PACK, T], F32, name=f"x_raw{s}") for s in range(PASSES)]
-        x_bf = [
-            sbuf_tile(f"x_bf{s}", [P, T, PACK], BF16, None)
-            for s in range(PASSES)
-        ]
+        x_raw = [sbuf_tile(f"x_raw{s}", [P, PACK, T], F32, RAW_PLACES[s]) for s in range(PASSES)]
+        x_bf = [sbuf_tile(f"x_bf{s}", [P, T, PACK], BF16, X_PLACES[s]) for s in range(PASSES)]
         token_codes = [sbuf_tile(f"token_codes{s}", [P, T], U32) for s in range(PASSES)]
-        token_plane01 = sbuf_tile("token_plane01", [P, T], U8)
-        token_plane2 = sbuf_tile("token_plane2", [P, T], U8)
-        token_plane3 = sbuf_tile("token_plane3", [P, T], U8)
-        token_scales = [token_plane01[:], token_plane01[4:, :], token_plane2[:], token_plane3[:]]
-        slot_plane01 = sbuf_tile("slot_plane01", [P, SLOTS], U8)
-        slot_plane1 = sbuf_tile("slot_plane1", [P, SLOTS], U8)
-        w1_planes = {
-            a: sbuf_tile(f"w1_planes{a}", [P, (b - a) * PASSES, H], U8)
-            for a, b in W1_SCALE_GROUPS
-        }
-        w2_planes = sbuf_tile("w2_planes", [P, E, N], U8)
-        y_out = keep.tile([P, N_TILES, RANKS, W2_PAIRS[-1][0], U], F32, name="y_out")
+        token_planes = [sbuf_tile(f"token_plane{g}", [P, T], U8) for g in range(PASSES - 1)]
+        token_scales = [token_planes[0][:], token_planes[0][4:, :], token_planes[1][:], token_planes[2][:]]
+        w1_planes = {a: sbuf_tile(f"w1_planes{a}", [P, (b - a) * PASSES, H], U8, RAW2_PLACE if a else None) for a, b in ((0, EARLY), (EARLY, E))}
+        w2_planes = sbuf_tile("w2_planes", [P, E, N], U8, W2_PLANES_PLACE)
+        y_out = keep.tile([P, N_TILES, RANKS, PAIRS[-1][0], U], F32, name="y_out")
         ident = keep.tile([P, P], F32, name="ident")
         slot_codes, slot_scales, w1_codes, w2_codes, h_mx = {}, {}, {}, {}, {}
 
-        for plane in (token_plane01, token_plane2, token_plane3):
+        for plane in token_planes:
             nc.gpsimd.memset(plane[:].bitcast(I32), 0)
         make_identity(nc, ident[:])
 
@@ -88,18 +80,17 @@ def tile_moe_eps_mlp_relu_kernel(tc, xT, w1_words, w1_scales, w2_words, w2_scale
             rows = xT[P * PACK * s : P * PACK * (s + 1), :]
             nc.sync.dma_start(x_raw[s][:], rows.rearrange("(p j) t -> p j t", j=PACK))
 
-        def load_w1(e, a, b, place=None):
-            words = sbuf_tile(f"w1_words{e}_{a}", [P, b - a, PASS_BYTES], U8, place)
+        def load_w1(e, a, b):
+            words = sbuf_tile(f"w1_words{e}_{a}", [P, b - a, PASS_BYTES], U8)
             nc.sync.dma_start(words[:].bitcast(I32), w1_words[e, a:b].rearrange("s p b -> p s b").bitcast(I32))
             for s in range(a, b):
                 w1_codes[e, s] = words[:, s - a, :]
 
-        def load_w1_pass(s):
-            place = FIRST * PASS_BYTES * s if s < 2 else None
-            words = sbuf_tile(f"w1_pass{s}", [P, FIRST, PASS_BYTES], U8, place)
-            nc.sync.dma_start(words[:].bitcast(I32), w1_words[0:FIRST, s].rearrange("e p b -> p e b").bitcast(I32))
-            for e in range(FIRST):
-                w1_codes[e, s] = words[:, e, :]
+        def load_w1_last_pass(a, b):
+            words = sbuf_tile(f"w1_last{a}", [P, b - a, PASS_BYTES], U8)
+            nc.sync.dma_start(words[:].bitcast(I32), w1_words[a:b, LAST_PASS].rearrange("e p b -> p e b").bitcast(I32))
+            for e in range(a, b):
+                w1_codes[e, LAST_PASS] = words[:, e - a, :]
 
         def load_w2(a, b):
             words = sbuf_tile(f"w2_words{a}", [P, b - a, 2 * N], U8)
@@ -111,13 +102,6 @@ def tile_moe_eps_mlp_relu_kernel(tc, xT, w1_words, w1_scales, w2_words, w2_scale
             view = scales.rearrange("e s (g r) i -> r g (e s) i", r=4)
             for r in range(4):
                 queue.dma_start(planes[r:P:32, :, :].bitcast(I32), view[r].bitcast(I32))
-
-        def load_early_scale_rows(a, b):
-            view = w1_scales[0 : W1_SCALE_GROUPS[0][1]].rearrange("e s q i -> q (e s) i")
-            for n in range(a, b):
-                q = n // 2 + SCALE_ROWS // 2 * (n % 2)
-                p = 32 * (q // 4) + q % 4
-                nc.sync.dma_start(w1_planes[0][p : p + 1, :, :].bitcast(I32), view[q : q + 1].bitcast(I32))
 
         def interleave(copy, s, a, b):
             copy(
@@ -146,6 +130,18 @@ def tile_moe_eps_mlp_relu_kernel(tc, xT, w1_words, w1_scales, w2_words, w2_scale
             for e in range(a, b):
                 slot_codes[e, s] = codes[:, C * (e - a) : C * (e - a + 1)]
 
+        def gather_shared_scales(s, groups, queue):
+            a, b = groups[0][0], groups[-1][1]
+            both = sbuf_tile(f"slot_scales{s}_{a}", [P, C * (b - a)], U8)
+            moved = sbuf_tile(f"slot_scales{s + 1}_{a}", [P, C * (b - a)], U8)
+            for c, d in groups:
+                nc.vector.tensor_copy(both[:, C * (c - a) : C * (d - a)], token_planes[s // 2][:].indirect(entries(c, d)))
+            for r in range(4):
+                queue.dma_start(moved[r:P:32, :].bitcast(I32), both[4 + r : P : 32, :].bitcast(I32))
+            for e in range(a, b):
+                slot_scales[e, s] = both[:, C * (e - a) : C * (e - a + 1)]
+                slot_scales[e, s + 1] = moved[:, C * (e - a) : C * (e - a + 1)]
+
         def gather_scales(s, a, b, place=None):
             scales = sbuf_tile(f"slot_scales{s}_{a}", [P, C * (b - a)], U8, place)
             nc.vector.tensor_copy(scales[:], token_scales[s].indirect(entries(a, b)))
@@ -159,20 +155,10 @@ def tile_moe_eps_mlp_relu_kernel(tc, xT, w1_words, w1_scales, w2_words, w2_scale
             gather_codes(LAST_PASS, e, e + 1, place + 9 * C)
             gather_scales(LAST_PASS, e, e + 1, place + 13 * C)
 
-        def gather_shared_plane():
-            for a, b in HALVES:
-                nc.vector.tensor_copy(slot_plane01[:, C * a : C * b], token_plane01[:].indirect(entries(a, b)))
-            nc.sync.dma_start(
-                slot_plane1[0:LIVE_ROWS, :].bitcast(I32), slot_plane01[4 : 4 + LIVE_ROWS, :].bitcast(I32)
-            )
-            for e in range(E):
-                slot_scales[e, 0] = slot_plane01[:, C * e : C * (e + 1)]
-                slot_scales[e, 1] = slot_plane1[:, C * e : C * (e + 1)]
-
         acc = [psum.tile([P, H], F32, name=f"acc{e}", tag=f"bank{e}") for e in range(E)]
 
         def first_layer(e, passes=range(PASSES)):
-            first = max(a for a, b in W1_SCALE_GROUPS if a <= e)
+            first = 0 if e < EARLY else EARLY
             for s in passes:
                 nc.tensor.matmul_mx(
                     out=acc[e][:],
@@ -192,7 +178,7 @@ def tile_moe_eps_mlp_relu_kernel(tc, xT, w1_words, w1_scales, w2_words, w2_scale
                 pairs = h[:].rearrange("c u p j -> c (u p j)").bitcast(F32)
                 for u in range(2):
                     nc.tensor.transpose(turned[:, e - a, u, :], pairs[:, P * u : P * (u + 1)], ident[:])
-            h_bf = sbuf_tile(f"h_bf{a}", [P, (b - a) * C * PACK], BF16, X2_PLACE if a == 0 else None)
+            h_bf = sbuf_tile(f"h_bf{a}", [P, (b - a) * C * PACK], BF16, TURNED_PLACE if a == 0 else None)
             copy = nc.vector.tensor_copy if a in VECTOR_TURNS else nc.scalar.copy
             copy(
                 out=h_bf[:].bitcast(F32).rearrange("p (e c u) -> p e c u", e=b - a, u=2),
@@ -247,52 +233,50 @@ def tile_moe_eps_mlp_relu_kernel(tc, xT, w1_words, w1_scales, w2_words, w2_scale
         nc.sync.dma_start(offsets[:], offs)
         for s in range(1, PASSES):
             load_x(s)
-            load_early_scale_rows(6 * (s - 1), min(6 * s, SCALE_ROWS))
-        load_w1_pass(0)
+        load_scale_rows(nc.sync, w1_planes[0], w1_scales[:EARLY])
 
         quantize_tokens(0)
         for a, b in HALVES:
             gather_codes(0, a, b)
         quantize_tokens(1)
-        gather_shared_plane()
-        for s in range(1, PASSES):
-            load_w1_pass(s)
+        load_w1(0, 0, LAST_PASS)
+        gather_shared_scales(0, HALVES, nc.sync)
+        load_w1(1, 0, LAST_PASS)
+        load_w1_last_pass(0, FIRST)
         for e in range(FIRST, LAST_EXPERT):
             load_w1(e, 0, PASSES)
-            if e == 2:
-                load_scale_rows(nc.sync, w1_planes[W1_SCALE_GROUPS[1][0]], w1_scales[W1_SCALE_GROUPS[1][0] : E])
-                load_scale_rows(nc.sync, w2_planes, w2_scales)
-            if e == 4:
-                load_w2(*W2_PAIRS[0])
+        load_w2(*PAIRS[0])
         load_w1(LAST_EXPERT, 0, LAST_PASS)
         load_w1(LAST_EXPERT, LAST_PASS, PASSES)
-        for a, b in W2_PAIRS[1:]:
+        for a, b in PAIRS[1:]:
             load_w2(a, b)
         gather_codes(1, *HALVES[0])
         quantize_tokens(2)
+        load_scale_rows(nc.gpsimd, w1_planes[EARLY], w1_scales[EARLY:])
+        load_scale_rows(nc.gpsimd, w2_planes, w2_scales)
         gather_codes(2, *HALVES[0])
         gather_scales(2, *HALVES[0])
         quantize_tokens(LAST_PASS)
-        for a, b in ((0, FIRST), (FIRST, EARLY)):
+        for a, b in ((0, 2), (2, 3)):
             gather_codes(LAST_PASS, a, b)
             gather_scales(LAST_PASS, a, b)
+        for e in range(3, LAST_EXPERT):
+            gather_late(e, X_LAST_PLACE + 14 * C * (e - 3))
 
-        for s in range(PASSES):
+        for passes in (range(LAST_PASS), (LAST_PASS,)):
             for e in range(FIRST):
-                first_layer(e, (s,))
-        for e in range(EARLY, LAST_EXPERT):
-            gather_late(e, 14 * C * (e - EARLY))
+                first_layer(e, passes)
         first_layer(2)
-        hidden(*W2_PAIRS[0])
-        gather_late(LAST_EXPERT, X2_PLACE)
+        hidden(*PAIRS[0])
+        gather_late(LAST_EXPERT, TURNED_PLACE)
         first_layer(3)
         first_layer(4)
-        hidden(*W2_PAIRS[1])
-        for e in range(*W2_PAIRS[0]):
+        hidden(*PAIRS[1])
+        for e in range(*PAIRS[0]):
             second_layer(e, *h_mx[e])
-        store(*W2_PAIRS[0])
+        store(*PAIRS[0])
         first_layer(5)
-        for e in range(*W2_PAIRS[1]):
+        for e in range(*PAIRS[1]):
             second_layer(e, *h_mx[e])
-        store(*W2_PAIRS[1])
-        last_second_layers(*W2_PAIRS[2])
+        store(*PAIRS[1])
+        last_second_layers(*PAIRS[2])

from contextlib import ExitStack

import concourse.mybir as mybir
from concourse.masks import make_identity

K, T, E, C, H, N = 2048, 640, 6, 128, 512, 384
RANKS = 2
P = 128
PACK = 4
PASSES = K // (P * PACK)
LAST_PASS = PASSES - 1
LAST_EXPERT = E - 1
SLOTS = E * C
U = C // RANKS
N_TILES = N // P
FLOPS = 2 * SLOTS * (K * H + H * N)

F32 = mybir.dt.float32
BF16 = mybir.dt.bfloat16
I32 = mybir.dt.int32
U32 = mybir.dt.uint32
U16 = mybir.dt.uint16
U8 = mybir.dt.uint8
FP8X4 = mybir.dt.float8_e4m3fn_x4
FP4X4 = mybir.dt.float4_e2m1fn_x4
RELU = mybir.ActivationFunctionType.Relu

VECTOR_TOKENS = ((0, 384), (384, T), None, None)
SCALAR_TOKENS = (((384, T),), ((0, 384),), ((0, 512), (512, T)), ((0, 512), (512, T)))
QUANTIZE_TOKENS = ((0, 512), (512, T))
HALVES = ((0, 3), (3, 6))
LIVE_ROWS = 100
FIRST = 2
PAIRS = ((0, 2), (2, 4), (4, 6))
PASS_BYTES = 2 * H
X_LAST_PLACE = 0
X_BYTES = 2 * PACK * T
X2_PLACE = X_BYTES
TURNED_PLACE = 2 * X_BYTES
RAW_BYTES = 4 * PACK * T
RAW2_PLACE = TURNED_PLACE + 2 * PASS_BYTES
RAW_PLACES = (None, None, RAW2_PLACE, None)
W2_PLANES_PLACE = RAW2_PLACE + 2 * PASSES * H
X_PLACES = (None, None, X2_PLACE, X_LAST_PLACE)
EARLY = 4
VECTOR_TURNS = (4,)
SCALAR_Y = (0, 2)
TURNED_BANK = {0: 1, 2: 3, 4: 6, 5: 7}


def tile_moe_eps_mlp_relu_kernel(tc, xT, w1_words, w1_scales, w2_words, w2_scales, offs, out):
    nc = tc.nc
    with ExitStack() as ctx:
        keep = ctx.enter_context(tc.tile_pool(name="keep", bufs=1))
        turns = ctx.enter_context(tc.tile_pool(name="turns", bufs=1))
        psum = ctx.enter_context(tc.psum_pool(name="psum", bufs=1))

        def sbuf_tile(name, shape, dtype, place=None):
            if place is None:
                return keep.tile(shape, dtype, name=name, align_bytes=64)
            return turns.tile(shape, dtype, name=name, align_bytes=64, offset=place)

        offsets = keep.tile([P, SLOTS // 16], U16, name="offsets")
        x_raw = [sbuf_tile(f"x_raw{s}", [P, PACK, T], F32, RAW_PLACES[s]) for s in range(PASSES)]
        x_bf = [sbuf_tile(f"x_bf{s}", [P, T, PACK], BF16, X_PLACES[s]) for s in range(PASSES)]
        token_codes = [sbuf_tile(f"token_codes{s}", [P, T], U32) for s in range(PASSES)]
        token_planes = [sbuf_tile(f"token_plane{g}", [P, T], U8) for g in range(PASSES - 1)]
        token_scales = [token_planes[0][:], token_planes[0][4:, :], token_planes[1][:], token_planes[2][:]]
        w1_planes = {a: sbuf_tile(f"w1_planes{a}", [P, (b - a) * PASSES, H], U8, RAW2_PLACE if a else None) for a, b in ((0, EARLY), (EARLY, E))}
        w2_planes = sbuf_tile("w2_planes", [P, E, N], U8, W2_PLANES_PLACE)
        y_out = keep.tile([P, N_TILES, RANKS, PAIRS[-1][0], U], F32, name="y_out")
        ident = keep.tile([P, P], F32, name="ident")
        slot_codes, slot_scales, w1_codes, w2_codes, h_mx = {}, {}, {}, {}, {}

        for plane in token_planes:
            nc.gpsimd.memset(plane[:].bitcast(I32), 0)
        make_identity(nc, ident[:])

        def load_x(s):
            rows = xT[P * PACK * s : P * PACK * (s + 1), :]
            nc.sync.dma_start(x_raw[s][:], rows.rearrange("(p j) t -> p j t", j=PACK))

        def load_w1(e, a, b):
            words = sbuf_tile(f"w1_words{e}_{a}", [P, b - a, PASS_BYTES], U8)
            nc.sync.dma_start(words[:].bitcast(I32), w1_words[e, a:b].rearrange("s p b -> p s b").bitcast(I32))
            for s in range(a, b):
                w1_codes[e, s] = words[:, s - a, :]

        def load_w1_last_pass(a, b):
            words = sbuf_tile(f"w1_last{a}", [P, b - a, PASS_BYTES], U8)
            nc.sync.dma_start(words[:].bitcast(I32), w1_words[a:b, LAST_PASS].rearrange("e p b -> p e b").bitcast(I32))
            for e in range(a, b):
                w1_codes[e, LAST_PASS] = words[:, e - a, :]

        def load_w2(a, b):
            words = sbuf_tile(f"w2_words{a}", [P, b - a, 2 * N], U8)
            nc.sync.dma_start(words[:].bitcast(I32), w2_words[a:b].rearrange("e s p b -> p (e s) b").bitcast(I32))
            for e in range(a, b):
                w2_codes[e] = words[:, e - a, :]

        def load_scale_rows(queue, planes, scales):
            view = scales.rearrange("e s (g r) i -> r g (e s) i", r=4)
            for r in range(4):
                queue.dma_start(planes[r:P:32, :, :].bitcast(I32), view[r].bitcast(I32))

        def interleave(copy, s, a, b):
            copy(
                out=x_bf[s][:, a:b, :].rearrange("p (c i) j -> p c j i", i=4),
                in_=x_raw[s][:, :, a:b].rearrange("p j (c i) -> p c j i", i=4),
            )

        def quantize_tokens(s):
            if VECTOR_TOKENS[s]:
                interleave(nc.vector.tensor_copy, s, *VECTOR_TOKENS[s])
            for a, b in SCALAR_TOKENS[s]:
                interleave(nc.scalar.copy, s, a, b)
            for a, b in QUANTIZE_TOKENS:
                nc.vector.quantize_mx(
                    out=token_codes[s][:, a:b].bitcast(FP8X4),
                    scales=token_scales[s][:, a:b],
                    in_=x_bf[s][:, a:b, :].rearrange("p t j -> p (t j)"),
                )

        def entries(a, b):
            return offsets[:, C * a // 16 : C * b // 16]

        def gather_codes(s, a, b, place=None):
            codes = sbuf_tile(f"slot_codes{s}_{a}", [P, C * (b - a)], U32, place)
            nc.vector.tensor_copy(codes[:], token_codes[s][:].indirect(entries(a, b)))
            for e in range(a, b):
                slot_codes[e, s] = codes[:, C * (e - a) : C * (e - a + 1)]

        def gather_shared_scales(s, groups, queue):
            a, b = groups[0][0], groups[-1][1]
            both = sbuf_tile(f"slot_scales{s}_{a}", [P, C * (b - a)], U8)
            moved = sbuf_tile(f"slot_scales{s + 1}_{a}", [P, C * (b - a)], U8)
            for c, d in groups:
                nc.vector.tensor_copy(both[:, C * (c - a) : C * (d - a)], token_planes[s // 2][:].indirect(entries(c, d)))
            for r in range(4):
                queue.dma_start(moved[r:P:32, :].bitcast(I32), both[4 + r : P : 32, :].bitcast(I32))
            for e in range(a, b):
                slot_scales[e, s] = both[:, C * (e - a) : C * (e - a + 1)]
                slot_scales[e, s + 1] = moved[:, C * (e - a) : C * (e - a + 1)]

        def gather_scales(s, a, b, place=None):
            scales = sbuf_tile(f"slot_scales{s}_{a}", [P, C * (b - a)], U8, place)
            nc.vector.tensor_copy(scales[:], token_scales[s].indirect(entries(a, b)))
            for e in range(a, b):
                slot_scales[e, s] = scales[:, C * (e - a) : C * (e - a + 1)]

        def gather_late(e, place):
            gather_codes(1, e, e + 1, place)
            gather_codes(2, e, e + 1, place + 4 * C)
            gather_scales(2, e, e + 1, place + 8 * C)
            gather_codes(LAST_PASS, e, e + 1, place + 9 * C)
            gather_scales(LAST_PASS, e, e + 1, place + 13 * C)

        acc = [psum.tile([P, H], F32, name=f"acc{e}", tag=f"bank{e}") for e in range(E)]

        def first_layer(e, passes=range(PASSES)):
            first = 0 if e < EARLY else EARLY
            for s in passes:
                nc.tensor.matmul_mx(
                    out=acc[e][:],
                    lhsT=slot_codes[e, s].bitcast(FP8X4),
                    lhsT_scale=slot_scales[e, s],
                    rhs=w1_codes[e, s].bitcast(FP4X4),
                    rhs_scale=w1_planes[first][:, PASSES * (e - first) + s, :],
                    start=(s == 0),
                    stop=(s == LAST_PASS),
                )

        def hidden(a, b):
            turned = psum.tile([P, b - a, 2, C], F32, name=f"turned{a}", tag=f"bank{TURNED_BANK[a]}")
            for e in range(a, b):
                h = sbuf_tile(f"h{e}", [P, 2, P, 2], BF16)
                nc.scalar.activation(out=h[:], in_=acc[e][:].rearrange("c (p u j) -> c u p j", u=2, j=2), func=RELU)
                pairs = h[:].rearrange("c u p j -> c (u p j)").bitcast(F32)
                for u in range(2):
                    nc.tensor.transpose(turned[:, e - a, u, :], pairs[:, P * u : P * (u + 1)], ident[:])
            h_bf = sbuf_tile(f"h_bf{a}", [P, (b - a) * C * PACK], BF16, TURNED_PLACE if a == 0 else None)
            copy = nc.vector.tensor_copy if a in VECTOR_TURNS else nc.scalar.copy
            copy(
                out=h_bf[:].bitcast(F32).rearrange("p (e c u) -> p e c u", e=b - a, u=2),
                in_=turned[:].rearrange("p e u c -> p e c u"),
            )
            codes = sbuf_tile(f"h_codes{a}", [P, (b - a) * C], U32)
            scales = sbuf_tile(f"h_scales{a}", [P, (b - a) * C], U8)
            nc.vector.quantize_mx(out=codes[:].bitcast(FP8X4), scales=scales[:], in_=h_bf[:])
            for e in range(a, b):
                h_mx[e] = codes[:, C * (e - a) : C * (e - a + 1)], scales[:, C * (e - a) : C * (e - a + 1)]

        def second_product(y, e, t, h_codes, h_scales):
            nc.tensor.matmul_mx(
                out=y,
                lhsT=w2_codes[e][:, 2 * P * t : 2 * P * (t + 1)].bitcast(FP4X4),
                lhsT_scale=w2_planes[:, e, P * t : P * (t + 1)],
                rhs=h_codes.bitcast(FP8X4),
                rhs_scale=h_scales,
                start=True,
                stop=True,
            )

        def second_layer(e, h_codes, h_scales):
            y = psum.tile([P, N_TILES, C], F32, name=f"y{e}", tag=f"bank{e}")
            for t in range(N_TILES):
                second_product(y[:, t, :], e, t, h_codes, h_scales)
            copy = nc.scalar.copy if e in SCALAR_Y else nc.vector.tensor_copy
            copy(out=y_out[:, :, :, e, :], in_=y[:].rearrange("p t (m u) -> p t m u", m=RANKS))

        def store(a, b):
            for m in range(RANKS):
                nc.sync.dma_start(
                    out[:, E * U * m + U * a : E * U * m + U * b].rearrange("(t p) c -> p t c", p=P),
                    y_out[:, :, m, a:b, :].rearrange("p t e u -> p t (e u)"),
                )

        def last_second_layers(a, b):
            for e in range(a, b):
                hidden(e, e + 1)
            ys = [psum.tile([P, b - a, C], F32, name=f"y_last{t}", tag=f"bank{(0, 1, a)[t]}") for t in range(N_TILES)]
            for e in range(a, b):
                for t in range(N_TILES):
                    second_product(ys[t][:, e - a, :], e, t, *h_mx[e])
            for t in range(N_TILES):
                rows = keep.tile([P, RANKS, b - a, U], F32, name=f"y_rows{t}")
                copy = nc.scalar.copy if t % 2 else nc.vector.tensor_copy
                copy(out=rows[:], in_=ys[t][:].rearrange("p e (m u) -> p m e u", m=RANKS))
                view = out[P * t : P * (t + 1), :].rearrange("p (m c) -> p m c", m=RANKS)
                nc.sync.dma_start(view[:, :, U * a : U * b], rows[:].rearrange("p m e u -> p m (e u)"))

        load_x(0)
        nc.sync.dma_start(offsets[:], offs)
        for s in range(1, PASSES):
            load_x(s)
        load_scale_rows(nc.sync, w1_planes[0], w1_scales[:EARLY])

        quantize_tokens(0)
        for a, b in HALVES:
            gather_codes(0, a, b)
        quantize_tokens(1)
        load_w1(0, 0, LAST_PASS)
        gather_shared_scales(0, HALVES, nc.sync)
        load_w1(1, 0, LAST_PASS)
        load_w1_last_pass(0, FIRST)
        for e in range(FIRST, LAST_EXPERT):
            load_w1(e, 0, PASSES)
        load_w2(*PAIRS[0])
        load_w1(LAST_EXPERT, 0, LAST_PASS)
        load_w1(LAST_EXPERT, LAST_PASS, PASSES)
        for a, b in PAIRS[1:]:
            load_w2(a, b)
        gather_codes(1, *HALVES[0])
        quantize_tokens(2)
        load_scale_rows(nc.gpsimd, w1_planes[EARLY], w1_scales[EARLY:])
        load_scale_rows(nc.gpsimd, w2_planes, w2_scales)
        gather_codes(2, *HALVES[0])
        gather_scales(2, *HALVES[0])
        quantize_tokens(LAST_PASS)
        for a, b in ((0, 2), (2, 3)):
            gather_codes(LAST_PASS, a, b)
            gather_scales(LAST_PASS, a, b)
        for e in range(3, LAST_EXPERT):
            gather_late(e, X_LAST_PLACE + 14 * C * (e - 3))

        for passes in (range(LAST_PASS), (LAST_PASS,)):
            for e in range(FIRST):
                first_layer(e, passes)
        first_layer(2)
        hidden(*PAIRS[0])
        gather_late(LAST_EXPERT, TURNED_PLACE)
        first_layer(3)
        first_layer(4)
        hidden(*PAIRS[1])
        for e in range(*PAIRS[0]):
            second_layer(e, *h_mx[e])
        store(*PAIRS[0])
        first_layer(5)
        for e in range(*PAIRS[1]):
            second_layer(e, *h_mx[e])
        store(*PAIRS[1])
        last_second_layers(*PAIRS[2])
